import numpy as np
import ml_dtypes


def mxq(x, axis, fmt="e4m3"):
    dtype, down = {"e4m3": (ml_dtypes.float8_e4m3fn, 7), "e5m2": (ml_dtypes.float8_e5m2, 14)}[fmt]
    v = np.moveaxis(np.asarray(x, np.float32).astype(ml_dtypes.bfloat16).astype(np.float64), axis, -1)
    blocks = v.reshape(v.shape[:-1] + (-1, 32))
    amax = np.abs(blocks).max(-1, keepdims=True)
    byte = np.maximum(np.where(amax > 0, np.frexp(amax)[1] - 1 + 127, 0) - down, 1)
    scale = np.exp2(byte - 127.0)
    codes = (blocks / scale).astype(np.float32).astype(dtype).astype(np.float64)
    return np.moveaxis((codes * scale).reshape(v.shape), -1, axis)


WIDE = False


def mx_kscale(k):
    if not WIDE:
        return np.ones(k)
    levels = np.array([10, -10, 5, -5, 0])
    if k % 512:
        return np.exp2(np.random.permutation(np.resize(levels, k // 32))).repeat(32)
    a = np.empty((k // 512, 16))
    for p in range(k // 512):
        a[p, :8] = np.random.permutation(np.resize(levels, 8))
        for g in range(8):
            far = levels[np.abs(levels - a[p, g]) >= 10]
            a[p, g + 8] = far[np.random.randint(len(far))]
    return np.exp2(a.ravel()).repeat(32)


def f64(x):
    return np.asarray(x).astype(np.float64)


def striped(idx):
    return np.tile(idx.reshape(-1, 16).T, (8, 1)).astype(np.uint16)


def unstriped(offs):
    return offs[:16].T.reshape(-1).astype(np.int64)


def pack_weight(w):
    k, n = w.shape
    w = f64(np.asarray(w, np.float32).astype(ml_dtypes.bfloat16)).reshape(k // 32, 32, n)
    amax = np.abs(w).max(1)
    byte = np.clip(np.where(amax > 0, np.frexp(amax)[1] - 1 + 127 - 7, 1), 1, 254)
    scaled = (w * np.exp2(127.0 - byte)[:, None, :]).reshape(k, n).astype(np.float32)
    words = np.ascontiguousarray(scaled.reshape(k // 512, 128, 4, n).transpose(0, 1, 3, 2)).astype(ml_dtypes.float8_e4m3fn).view(np.uint8)
    return words, np.ascontiguousarray(byte.astype(np.uint8).reshape(k // 512, 16, n))


def unpack_weight(words, scales):
    g, p, n, _ = words.shape
    vals = np.ascontiguousarray(words).view(ml_dtypes.float8_e4m3fn).astype(np.float64) * np.repeat(np.exp2(scales.astype(np.float64) - 127.0), 8, axis=1)[..., None]
    return vals.transpose(0, 1, 3, 2).reshape(g * 512, n)


def planes(y):
    n, m = y.shape
    v = y.astype(np.float32).astype(ml_dtypes.bfloat16).astype(np.float64).reshape(n // 32, 32, m)
    top = np.abs(v).max(1)
    byte = np.clip(np.where(top > 0, np.frexp(top)[1] - 1 + 127 - 7, 1), 1, 254)
    codes = (v * np.exp2(127.0 - byte)[:, None, :]).reshape(n, m).astype(np.float32).astype(ml_dtypes.float8_e4m3fn).view(np.uint8)
    words = codes.reshape(n // 512, 128, 4, m).transpose(0, 1, 3, 2)
    return np.ascontiguousarray(words), np.ascontiguousarray(byte.astype(np.uint8).reshape(n // 512, 16, m))


K, T, S, H, N = 1024, 2048, 512, 512, 512


def setup_inputs():
    n = np.random.standard_normal
    s = mx_kscale(K)[:, None]
    u = mx_kscale(H)
    near = np.random.permutation(S)
    packed_xT = pack_weight(n((K, T)) * s)
    return {
        "x_words": packed_xT[0],
        "x_scales": packed_xT[1],
        "w1": (n((K, H)) / np.sqrt(K) / s * u).astype(np.float32),
        "w2": (n((H, N)) / np.sqrt(H) / u[:, None]).astype(np.float32),
        "taps": (0.6 * n((H, 3))).astype(np.float32),
        "offs": striped(np.random.permutation(T)[:S]),
        "order": striped(near),
        "back": striped(np.argsort(near)),
    }


def reference(x_words, x_scales, w1, w2, taps, offs, order, back):
    xq = unpack_weight(x_words, x_scales)[:, unstriped(offs)]
    y = mxq(f64(w1), 0, "e4m3").T @ xq
    gg = y[:, unstriped(order)]
    rr = f64(taps)[:, 0:1] * gg + f64(taps)[:, 1:2] * (np.pad(gg, ((0, 0), (1, 0)))[:, :S]) + f64(taps)[:, 2:3] * (np.pad(gg, ((0, 0), (2, 0)))[:, :S])
    z = rr[:, unstriped(back)] + y
    out_0 = mxq(f64(w2), 0, "e4m3").T @ mxq(z, 0, "e4m3")
    return (out_0,) + planes(out_0)

@@ -1,0 +1,233 @@
+from contextlib import ExitStack
+
+import concourse.mybir as mybir
+
+K, T, S, H, N = 1024, 2048, 512, 512, 512
+FLOPS = 2 * K * H * S + 2 * H * N * S
+
+F32 = mybir.dt.float32
+BF16 = mybir.dt.bfloat16
+I32 = mybir.dt.int32
+U32 = mybir.dt.uint32
+U16 = mybir.dt.uint16
+U8 = mybir.dt.uint8
+FP8X4 = mybir.dt.float8_e4m3fn_x4
+COPY = mybir.ActivationFunctionType.Copy
+MULT = mybir.AluOpType.mult
+ADD = mybir.AluOpType.add
+
+P = 128
+PACK = 4
+K_PASS = P * PACK
+PASSES = K // K_PASS
+Y_WINDOW = 704
+LEAD = 4
+PIECES = ((0, 256), (256, 384), (384, 512))
+W1_SPLIT = 80
+
+
+def deal(engine_copy, grouped, raw, m0, m1, base=0):
+    engine_copy(
+        out=grouped[:].rearrange("p (t m j) -> p m j t", t=PACK, j=PACK)[:, m0:m1],
+        in_=raw[:].rearrange("p j (m t) -> p m j t", t=PACK)[:, m0 - base : m1 - base],
+    )
+
+
+def weave(engine_copy, woven, planes):
+    engine_copy(
+        out=woven.rearrange("p (c i t) -> p c t i", t=PACK, i=4),
+        in_=planes.rearrange("p t (c i) -> p c t i", i=4),
+    )
+
+
+def tile_picked_yserial_none_po_kernel(
+    tc, x_words, x_scales, w1, w2, taps, offs, order, back, out_0, out_1, out_2
+):
+    nc = tc.nc
+    with ExitStack() as ctx:
+        lists = ctx.enter_context(tc.tile_pool(name="lists", bufs=1))
+        keep = ctx.enter_context(tc.tile_pool(name="keep", bufs=1))
+        psum = ctx.enter_context(tc.psum_pool(name="psum", bufs=1))
+
+        offs_sb = lists.tile([P, S // 16], U16, name="offs_sb")
+        order_sb = lists.tile([P, S // 16], U16, name="order_sb")
+        back_sb = lists.tile([P, S // 16], U16, name="back_sb")
+
+        scale_table = keep.tile([P, T], U8, name="scale_table", align_bytes=64)
+        word_table = [keep.tile([P, T], U32, name="word_table%d" % o, align_bytes=64) for o in range(PASSES)]
+        w1_raw = [keep.tile([P, PACK, H], F32, name="w1_raw%d" % o, align_bytes=64) for o in range(PASSES)]
+        w2_raw = [keep.tile([P, PACK, N // 2], F32, name="w2_raw%d" % h, align_bytes=64) for h in range(2)]
+        taps_sb = keep.tile([P, PACK, 3], F32, name="taps_sb")
+
+        nc.gpsimd.memset(scale_table[:].bitcast(I32), 0)
+        for q in range(4):
+            nc.gpsimd.dma_start(
+                out=scale_table[32 * q : 32 * q + 4 * PASSES, :].bitcast(I32),
+                in_=x_scales[:, 4 * q : 4 * q + 4, :].bitcast(I32),
+            )
+        for o in range(PASSES):
+            nc.sync.dma_start(
+                out=w1_raw[o][:], in_=w1[o * K_PASS : (o + 1) * K_PASS, :].rearrange("(p j) c -> p j c", j=PACK)
+            )
+            if o == 0:
+                nc.sync.dma_start(out=offs_sb[:], in_=offs)
+            nc.sync.dma_start(
+                out=word_table[o][:].bitcast(I32), in_=x_words[o].rearrange("p c r -> p (c r)").bitcast(I32)
+            )
+        nc.sync.dma_start(out=taps_sb[:], in_=taps.rearrange("(p t) e -> p t e", t=PACK))
+        nc.sync.dma_start(out=order_sb[:], in_=order)
+        nc.sync.dma_start(out=back_sb[:], in_=back)
+        for h in range(2):
+            nc.sync.dma_start(
+                out=w2_raw[h][:], in_=w2.rearrange("(p j) c -> p j c", j=PACK)[:, :, h * 256 : (h + 1) * 256]
+            )
+
+        y = [keep.tile([P, Y_WINDOW], F32, name="y%d" % t, align_bytes=64) for t in range(PACK)]
+        gg = [keep.tile([P, LEAD + S], F32, name="gg%d" % t, align_bytes=64) for t in range(PACK)]
+        for t in range(PACK):
+            nc.vector.memset(y[t][:, S:Y_WINDOW], 0.0)
+            nc.vector.memset(gg[t][:, 0:LEAD], 0.0)
+
+        x_code = [keep.tile([P, S], U32, name="x_code%d" % o, align_bytes=64) for o in range(PASSES)]
+        w1_code = [keep.tile([P, H], U32, name="w1_code%d" % o, align_bytes=64) for o in range(PASSES)]
+        w1_scale = [keep.tile([P, H], U8, name="w1_scale%d" % o, align_bytes=64) for o in range(PASSES)]
+        w1_bf = [keep.tile([P, PACK * H], BF16, name="w1_bf%d" % o, tag="w1_bf%d" % o, align_bytes=64) for o in range(PASSES)]
+        y_parts = [(0, 0, 256), (0, 256, 512), (1, 0, 512), (2, 0, 512), (3, 0, 512)]
+        y_ps = [psum.tile([P, b - a], F32, name="y_ps%d" % n, tag="y_ps%d" % n) for n, (t, a, b) in enumerate(y_parts)]
+        w2_bf = keep.tile([P, PACK * N], BF16, name="w2_bf", align_bytes=64)
+
+        for o in range(PASSES):
+            deal(nc.vector.tensor_copy, w1_bf[o], w1_raw[o], 0, W1_SPLIT)
+            deal(nc.scalar.copy, w1_bf[o], w1_raw[o], W1_SPLIT, P)
+            nc.vector.quantize_mx(out=w1_code[o][:].bitcast(FP8X4), scales=w1_scale[o][:], in_=w1_bf[o][:])
+            if o == 0:
+                nc.vector.tensor_copy(out=x_code[o][:], in_=word_table[o][:].indirect(offs_sb[:]))
+                x_scale = keep.tile([P, S], U8, name="x_scale", tag="w1_bf0", align_bytes=64)
+                nc.vector.tensor_copy(out=x_scale[:], in_=scale_table[:].indirect(offs_sb[:]))
+            else:
+                for h in range(2):
+                    nc.vector.tensor_copy(
+                        out=x_code[o][:, h * 256 : (h + 1) * 256],
+                        in_=word_table[o][:].indirect(offs_sb[:, h * 16 : (h + 1) * 16]),
+                    )
+            for n, (t, a, b) in enumerate(y_parts):
+                cols = slice(t * P, (t + 1) * P)
+                nc.tensor.matmul_mx(
+                    out=y_ps[n][:],
+                    lhsT=w1_code[o][:, cols].bitcast(FP8X4),
+                    lhsT_scale=w1_scale[o][:, cols],
+                    rhs=x_code[o][:, a:b].bitcast(FP8X4),
+                    rhs_scale=x_scale[4 * o : P, a:b],
+                    start=(o == 0),
+                    stop=(o == PASSES - 1),
+                )
+
+        keep_gain = keep.tile([P, PACK], F32, name="keep_gain")
+        nc.scalar.activation(out=keep_gain[:], in_=taps_sb[:, :, 0], func=COPY, bias=1.0)
+
+        y_kept = [keep.tile([P, S], F32, name="y_kept%d" % t, align_bytes=64) for t in range(PACK)]
+        far = [keep.tile([P, S], F32, name="far%d" % t, align_bytes=64) for t in range(PACK)]
+        rr = [keep.tile([P, S], F32, name="rr%d" % t, align_bytes=64) for t in range(PACK)]
+        w2_code = keep.tile([P, N], U32, name="w2_code", align_bytes=64)
+        w2_scale = keep.tile([P, N], U8, name="w2_scale", align_bytes=64)
+
+        def filter_sum(t):
+            nc.vector.scalar_tensor_tensor(
+                out=rr[t][:], in0=gg[t][:, LEAD - 1 : LEAD - 1 + S], scalar=taps_sb[:, t, 1:2], in1=far[t][:],
+                op0=MULT, op1=ADD,
+            )
+
+        deal(nc.vector.tensor_copy, w2_bf, w2_raw[0], 0, 64)
+        for n, (t, a, b) in enumerate(y_parts):
+            nc.scalar.copy(out=y[t][:, a:b], in_=y_ps[n][:])
+        for t in range(PACK):
+            nc.vector.tensor_copy(out=gg[t][:, LEAD : LEAD + S], in_=y[t][:].indirect(order_sb[:]))
+            nc.scalar.activation(
+                out=far[t][:], in_=gg[t][:, LEAD - 2 : LEAD - 2 + S], func=COPY, scale=taps_sb[:, t, 2:3]
+            )
+            for n, (owner, a, b) in enumerate(y_parts):
+                if owner == t:
+                    nc.scalar.activation(
+                        out=y_kept[t][:, a:b], in_=y_ps[n][:], func=COPY, scale=keep_gain[:, t : t + 1]
+                    )
+            if t >= 2:
+                deal(nc.scalar.copy, w2_bf, w2_raw[1], t * 32, (t + 1) * 32, base=64)
+            if t > 0:
+                filter_sum(t - 1)
+
+        z = [keep.tile([P, PACK, b - a], F32, name="z%d" % a, align_bytes=64)[:] for a, b in PIECES[:2]]
+        shared = keep.tile([P, 768], F32, name="shared", align_bytes=64)
+        last_bf = keep.tile([P, 512], BF16, name="last_bf", align_bytes=64)
+        z_bf = [shared[:, 0:512].bitcast(BF16), shared[:, 512:768].bitcast(BF16), last_bf[:]]
+        z.append(shared[:, 256:768].rearrange("p (t c) -> p t c", t=PACK))
+        z_code = [keep.tile([P, b - a], U32, name="z_code%d" % a, align_bytes=64) for a, b in PIECES]
+        z_scale = [keep.tile([P, b - a], U8, name="z_scale%d" % a, align_bytes=64) for a, b in PIECES]
+        res = [keep.tile([P, PACK, b - a], F32, name="res%d" % a, align_bytes=64) for a, b in PIECES]
+        res_bf = [keep.tile([P, PACK * (b - a)], BF16, name="res_bf%d" % a, align_bytes=64) for a, b in PIECES]
+        res_code = [keep.tile([P, b - a], U32, name="res_code%d" % a, align_bytes=64) for a, b in PIECES]
+        res_scale = keep.tile([P, S], U8, name="res_scale", align_bytes=64)
+        out_rows = out_0.rearrange("(p t) j -> p t j", t=PACK)
+        out_words = out_1[0].rearrange("p c r -> p (c r)").bitcast(I32)
+
+        def bring_back(i, t):
+            a, b = PIECES[i]
+            nc.vector.tensor_tensor(
+                out=z[i][:, t, :], in0=rr[t][:].indirect(back_sb[:, a // 16 : b // 16]), in1=y_kept[t][:, a:b], op=ADD
+            )
+
+        def round_z(i):
+            weave(nc.vector.tensor_copy if i == 2 else nc.scalar.copy, z_bf[i], z[i])
+
+        def second_product(i):
+            a, b = PIECES[i]
+            width = b - a
+            nc.vector.quantize_mx(out=z_code[i][:].bitcast(FP8X4), scales=z_scale[i][:], in_=z_bf[i])
+            per_bank = 4 if i == 1 else 2
+            for t0 in range(0, PACK, per_bank):
+                tag = "y_ps%d" % (t0 // 2) if i == 2 else "res_ps%d_%d" % (a, t0)
+                bank = psum.tile([P, per_bank, width], F32, name="res_ps%d_%d" % (a, t0), tag=tag)
+                for t in range(t0, t0 + per_bank):
+                    cols = slice(t * P, (t + 1) * P)
+                    nc.tensor.matmul_mx(
+                        out=bank[:, t - t0, :],
+                        lhsT=w2_code[:, cols].bitcast(FP8X4),
+                        lhsT_scale=w2_scale[:, cols],
+                        rhs=z_code[i][:].bitcast(FP8X4),
+                        rhs_scale=z_scale[i][:],
+                        start=True,
+                        stop=True,
+                    )
+                copy = nc.vector.tensor_copy if (i, t0) == (2, 2) else nc.scalar.copy
+                copy(out=res[i][:, t0 : t0 + per_bank, :], in_=bank[:])
+            nc.sync.dma_start(out=out_rows[:, :, a:b], in_=res[i][:])
+
+        def hand_on(i):
+            a, b = PIECES[i]
+            weave(nc.vector.tensor_copy, res_bf[i][:], res[i][:])
+            nc.vector.quantize_mx(out=res_code[i][:].bitcast(FP8X4), scales=res_scale[:, a:b], in_=res_bf[i][:])
+            nc.sync.dma_start(out=out_words[:, a:b], in_=res_code[i][:].bitcast(I32))
+
+        bring_back(0, 0)
+        filter_sum(PACK - 1)
+        for t in range(1, PACK):
+            bring_back(0, t)
+        round_z(0)
+        nc.vector.quantize_mx(out=w2_code[:].bitcast(FP8X4), scales=w2_scale[:], in_=w2_bf[:])
+        for t in range(PACK):
+            bring_back(1, t)
+        round_z(1)
+        second_product(0)
+        bring_back(2, 0)
+        bring_back(2, 1)
+        second_product(1)
+        bring_back(2, 2)
+        bring_back(2, 3)
+        round_z(2)
+        second_product(2)
+        for i in range(len(PIECES)):
+            hand_on(i)
+        for q in range(4):
+            queue = nc.scalar if q % 2 else nc.sync
+            queue.dma_start(
+                out=out_2[0, 4 * q : 4 * q + 4, :].bitcast(I32), in_=res_scale[32 * q : 32 * q + 4, :].bitcast(I32)
+            )

@@ -23,20 +23,20 @@ PASSES = K // K_PASS
 Y_WINDOW = 704
 LEAD = 4
 PIECES = ((0, 256), (256, 384), (384, 512))
-W1_SPLIT = 80
+W1_SPLIT = 72
 
 
 def deal(engine_copy, grouped, raw, m0, m1, base=0):
     engine_copy(
-        out=grouped[:].rearrange("p (t m j) -> p m j t", t=PACK, j=PACK)[:, m0:m1],
-        in_=raw[:].rearrange("p j (m t) -> p m j t", t=PACK)[:, m0 - base : m1 - base],
+        out=grouped[:].rearrange("p (t m j) -> p m t j", t=PACK, j=PACK)[:, m0:m1],
+        in_=raw[:].rearrange("p j (m t) -> p m t j", t=PACK)[:, m0 - base : m1 - base],
     )
 
 
 def weave(engine_copy, woven, planes):
     engine_copy(
-        out=woven.rearrange("p (c i t) -> p c t i", t=PACK, i=4),
-        in_=planes.rearrange("p t (c i) -> p c t i", i=4),
+        out=woven.rearrange("p (c t) -> p c t", t=PACK),
+        in_=planes.rearrange("p t c -> p c t"),
     )
 
 
@@ -60,27 +60,29 @@ def tile_picked_yserial_none_po_kernel(
         taps_sb = keep.tile([P, PACK, 3], F32, name="taps_sb")
 
         nc.gpsimd.memset(scale_table[:].bitcast(I32), 0)
-        for q in range(4):
-            nc.gpsimd.dma_start(
-                out=scale_table[32 * q : 32 * q + 4 * PASSES, :].bitcast(I32),
-                in_=x_scales[:, 4 * q : 4 * q + 4, :].bitcast(I32),
-            )
-        for o in range(PASSES):
+        def load_w1(o):
             nc.sync.dma_start(
                 out=w1_raw[o][:], in_=w1[o * K_PASS : (o + 1) * K_PASS, :].rearrange("(p j) c -> p j c", j=PACK)
             )
-            if o == 0:
-                nc.sync.dma_start(out=offs_sb[:], in_=offs)
+
+        load_w1(0)
+        for q in range(4):
+            nc.sync.dma_start(
+                out=scale_table[32 * q : 32 * q + 4 * PASSES, :].bitcast(I32),
+                in_=x_scales[:, 4 * q : 4 * q + 4, :].bitcast(I32),
+            )
+        nc.sync.dma_start(out=offs_sb[:], in_=offs)
+        nc.sync.dma_start(out=taps_sb[:], in_=taps.rearrange("(p t) e -> p t e", t=PACK))
+        load_w1(1)
+        for o in range(PASSES):
             nc.sync.dma_start(
                 out=word_table[o][:].bitcast(I32), in_=x_words[o].rearrange("p c r -> p (c r)").bitcast(I32)
             )
-        nc.sync.dma_start(out=taps_sb[:], in_=taps.rearrange("(p t) e -> p t e", t=PACK))
+        w2_rows = w2.rearrange("(p j) c -> p j c", j=PACK)
+        nc.sync.dma_start(out=w2_raw[0][:], in_=w2_rows[:, :, 0:256])
         nc.sync.dma_start(out=order_sb[:], in_=order)
         nc.sync.dma_start(out=back_sb[:], in_=back)
-        for h in range(2):
-            nc.sync.dma_start(
-                out=w2_raw[h][:], in_=w2.rearrange("(p j) c -> p j c", j=PACK)[:, :, h * 256 : (h + 1) * 256]
-            )
+        nc.sync.dma_start(out=w2_raw[1][:], in_=w2_rows[:, :, 256:512])
 
         y = [keep.tile([P, Y_WINDOW], F32, name="y%d" % t, align_bytes=64) for t in range(PACK)]
         gg = [keep.tile([P, LEAD + S], F32, name="gg%d" % t, align_bytes=64) for t in range(PACK)]
@@ -96,14 +98,15 @@ def tile_picked_yserial_none_po_kernel(
         y_ps = [psum.tile([P, b - a], F32, name="y_ps%d" % n, tag="y_ps%d" % n) for n, (t, a, b) in enumerate(y_parts)]
         w2_bf = keep.tile([P, PACK * N], BF16, name="w2_bf", align_bytes=64)
 
+        x_scale = keep.tile([P, S], U8, name="x_scale", align_bytes=64)
         for o in range(PASSES):
             deal(nc.vector.tensor_copy, w1_bf[o], w1_raw[o], 0, W1_SPLIT)
             deal(nc.scalar.copy, w1_bf[o], w1_raw[o], W1_SPLIT, P)
             nc.vector.quantize_mx(out=w1_code[o][:].bitcast(FP8X4), scales=w1_scale[o][:], in_=w1_bf[o][:])
+        nc.vector.tensor_copy(out=x_scale[:], in_=scale_table[:].indirect(offs_sb[:]))
+        for o in range(PASSES):
             if o == 0:
                 nc.vector.tensor_copy(out=x_code[o][:], in_=word_table[o][:].indirect(offs_sb[:]))
-                x_scale = keep.tile([P, S], U8, name="x_scale", tag="w1_bf0", align_bytes=64)
-                nc.vector.tensor_copy(out=x_scale[:], in_=scale_table[:].indirect(offs_sb[:]))
             else:
                 for h in range(2):
                     nc.vector.tensor_copy(
@@ -157,13 +160,12 @@ def tile_picked_yserial_none_po_kernel(
 
         z = [keep.tile([P, PACK, b - a], F32, name="z%d" % a, align_bytes=64)[:] for a, b in PIECES[:2]]
         shared = keep.tile([P, 768], F32, name="shared", align_bytes=64)
-        last_bf = keep.tile([P, 512], BF16, name="last_bf", align_bytes=64)
+        last_bf = keep.tile([P, 512], BF16, name="last_bf", tag="late", align_bytes=64)
         z_bf = [shared[:, 0:512].bitcast(BF16), shared[:, 512:768].bitcast(BF16), last_bf[:]]
         z.append(shared[:, 256:768].rearrange("p (t c) -> p t c", t=PACK))
         z_code = [keep.tile([P, b - a], U32, name="z_code%d" % a, align_bytes=64) for a, b in PIECES]
         z_scale = [keep.tile([P, b - a], U8, name="z_scale%d" % a, align_bytes=64) for a, b in PIECES]
         res = [keep.tile([P, PACK, b - a], F32, name="res%d" % a, align_bytes=64) for a, b in PIECES]
-        res_bf = [keep.tile([P, PACK * (b - a)], BF16, name="res_bf%d" % a, align_bytes=64) for a, b in PIECES]
         res_code = [keep.tile([P, b - a], U32, name="res_code%d" % a, align_bytes=64) for a, b in PIECES]
         res_scale = keep.tile([P, S], U8, name="res_scale", align_bytes=64)
         out_rows = out_0.rearrange("(p t) j -> p t j", t=PACK)
@@ -197,14 +199,15 @@ def tile_picked_yserial_none_po_kernel(
                         start=True,
                         stop=True,
                     )
-                copy = nc.vector.tensor_copy if (i, t0) == (2, 2) else nc.scalar.copy
-                copy(out=res[i][:, t0 : t0 + per_bank, :], in_=bank[:])
+                nc.scalar.copy(out=res[i][:, t0 : t0 + per_bank, :], in_=bank[:])
             nc.sync.dma_start(out=out_rows[:, :, a:b], in_=res[i][:])
 
         def hand_on(i):
             a, b = PIECES[i]
-            weave(nc.vector.tensor_copy, res_bf[i][:], res[i][:])
-            nc.vector.quantize_mx(out=res_code[i][:].bitcast(FP8X4), scales=res_scale[:, a:b], in_=res_bf[i][:])
+            tag = "late" if i == 0 else "res_bf%d" % a
+            res_bf = keep.tile([P, PACK * (b - a)], BF16, name="res_bf%d" % a, tag=tag, align_bytes=64)
+            weave(nc.scalar.copy if i == 1 else nc.vector.tensor_copy, res_bf[:], res[i][:])
+            nc.vector.quantize_mx(out=res_code[i][:].bitcast(FP8X4), scales=res_scale[:, a:b], in_=res_bf[:])
             nc.sync.dma_start(out=out_words[:, a:b], in_=res_code[i][:].bitcast(I32))
 
         bring_back(0, 0)

@@ -33,6 +33,10 @@ def deal(engine_copy, grouped, raw, m0, m1, base=0):
     )
 
 
+def scalar_cast(nc):
+    return lambda out, in_: nc.scalar.activation(out=out, in_=in_, func=COPY)
+
+
 def weave(engine_copy, woven, planes):
     engine_copy(
         out=woven.rearrange("p (c t) -> p c t", t=PACK),
@@ -65,19 +69,27 @@ def tile_picked_yserial_none_po_kernel(
                 out=w1_raw[o][:], in_=w1[o * K_PASS : (o + 1) * K_PASS, :].rearrange("(p j) c -> p j c", j=PACK)
             )
 
-        load_w1(0)
-        for q in range(4):
+        def load_scales(o, q):
+            row = 32 * q + 4 * o
             nc.sync.dma_start(
-                out=scale_table[32 * q : 32 * q + 4 * PASSES, :].bitcast(I32),
-                in_=x_scales[:, 4 * q : 4 * q + 4, :].bitcast(I32),
+                out=scale_table[row : row + 4, :].bitcast(I32), in_=x_scales[o, 4 * q : 4 * q + 4, :].bitcast(I32)
             )
-        nc.sync.dma_start(out=offs_sb[:], in_=offs)
-        nc.sync.dma_start(out=taps_sb[:], in_=taps.rearrange("(p t) e -> p t e", t=PACK))
-        load_w1(1)
-        for o in range(PASSES):
+
+        def load_words(o):
             nc.sync.dma_start(
                 out=word_table[o][:].bitcast(I32), in_=x_words[o].rearrange("p c r -> p (c r)").bitcast(I32)
             )
+
+        load_w1(0)
+        for q in range(4):
+            load_scales(0, q)
+        nc.sync.dma_start(out=offs_sb[:], in_=offs)
+        load_words(0)
+        nc.sync.dma_start(out=taps_sb[:], in_=taps.rearrange("(p t) e -> p t e", t=PACK))
+        for q in range(4):
+            load_scales(1, q)
+        load_w1(1)
+        load_words(1)
         w2_rows = w2.rearrange("(p j) c -> p j c", j=PACK)
         nc.sync.dma_start(out=w2_raw[0][:], in_=w2_rows[:, :, 0:256])
         nc.sync.dma_start(out=order_sb[:], in_=order)
@@ -101,12 +113,11 @@ def tile_picked_yserial_none_po_kernel(
         x_scale = keep.tile([P, S], U8, name="x_scale", align_bytes=64)
         for o in range(PASSES):
             deal(nc.vector.tensor_copy, w1_bf[o], w1_raw[o], 0, W1_SPLIT)
-            deal(nc.scalar.copy, w1_bf[o], w1_raw[o], W1_SPLIT, P)
+            deal(scalar_cast(nc), w1_bf[o], w1_raw[o], W1_SPLIT, P)
             nc.vector.quantize_mx(out=w1_code[o][:].bitcast(FP8X4), scales=w1_scale[o][:], in_=w1_bf[o][:])
-        nc.vector.tensor_copy(out=x_scale[:], in_=scale_table[:].indirect(offs_sb[:]))
-        for o in range(PASSES):
             if o == 0:
                 nc.vector.tensor_copy(out=x_code[o][:], in_=word_table[o][:].indirect(offs_sb[:]))
+                nc.vector.tensor_copy(out=x_scale[:], in_=scale_table[:].indirect(offs_sb[:]))
             else:
                 for h in range(2):
                     nc.vector.tensor_copy(
@@ -143,20 +154,25 @@ def tile_picked_yserial_none_po_kernel(
         deal(nc.vector.tensor_copy, w2_bf, w2_raw[0], 0, 64)
         for n, (t, a, b) in enumerate(y_parts):
             nc.scalar.copy(out=y[t][:, a:b], in_=y_ps[n][:])
-        for t in range(PACK):
-            nc.vector.tensor_copy(out=gg[t][:, LEAD : LEAD + S], in_=y[t][:].indirect(order_sb[:]))
-            nc.scalar.activation(
-                out=far[t][:], in_=gg[t][:, LEAD - 2 : LEAD - 2 + S], func=COPY, scale=taps_sb[:, t, 2:3]
-            )
+        def keep_own(t):
             for n, (owner, a, b) in enumerate(y_parts):
                 if owner == t:
                     nc.scalar.activation(
                         out=y_kept[t][:, a:b], in_=y_ps[n][:], func=COPY, scale=keep_gain[:, t : t + 1]
                     )
-            if t >= 2:
-                deal(nc.scalar.copy, w2_bf, w2_raw[1], t * 32, (t + 1) * 32, base=64)
+
+        for t in range(PACK):
+            nc.vector.tensor_copy(out=gg[t][:, LEAD : LEAD + S], in_=y[t][:].indirect(order_sb[:]))
+            nc.scalar.activation(
+                out=far[t][:], in_=gg[t][:, LEAD - 2 : LEAD - 2 + S], func=COPY, scale=taps_sb[:, t, 2:3]
+            )
+            if t in (1, 2):
+                keep_own(t - 1)
             if t > 0:
                 filter_sum(t - 1)
+        keep_own(2)
+        keep_own(3)
+        deal(nc.scalar.copy, w2_bf, w2_raw[1], 64, 128, base=64)
 
         z = [keep.tile([P, PACK, b - a], F32, name="z%d" % a, align_bytes=64)[:] for a, b in PIECES[:2]]
         shared = keep.tile([P, 768], F32, name="shared", align_bytes=64)

@@ -22,8 +22,14 @@ K_PASS = P * PACK
 PASSES = K // K_PASS
 Y_WINDOW = 704
 LEAD = 4
-PIECES = ((0, 256), (256, 384), (384, 512))
+PIECES = ((0, 64), (64, 192), (192, 320), (320, 448), (448, 512))
+STORES = PIECES
+HANDED = ((0, 256), (256, 512))
+CODE_STORES = ((0, 512),)
+GROUPS = PIECES
+X_CUTS = ((0, 256), (256, 512))
 W1_SPLIT = 72
+HALF_SPLITS = (24, 40)
 
 
 def deal(engine_copy, grouped, raw, m0, m1, base=0):
@@ -44,6 +50,13 @@ def weave(engine_copy, woven, planes):
     )
 
 
+def weave_by_lines(engine_copy, woven, planes):
+    engine_copy(
+        out=woven.rearrange("p (c i t) -> p c t i", i=4, t=PACK),
+        in_=planes.rearrange("p t (c i) -> p c t i", i=4),
+    )
+
+
 def tile_picked_yserial_none_po_kernel(
     tc, x_words, x_scales, w1, w2, taps, offs, order, back, out_0, out_1, out_2
 ):
@@ -59,20 +72,17 @@ def tile_picked_yserial_none_po_kernel(
 
         scale_table = keep.tile([P, T], U8, name="scale_table", align_bytes=64)
         word_table = [keep.tile([P, T], U32, name="word_table%d" % o, align_bytes=64) for o in range(PASSES)]
-        w1_raw = [keep.tile([P, PACK, H], F32, name="w1_raw%d" % o, align_bytes=64) for o in range(PASSES)]
+        w1_first = keep.tile([P, PACK, H], F32, name="w1_first", align_bytes=64)
+        w1_last = [keep.tile([P, PACK, H // 2], F32, name="w1_last%d" % h, align_bytes=64) for h in range(2)]
         w2_raw = [keep.tile([P, PACK, N // 2], F32, name="w2_raw%d" % h, align_bytes=64) for h in range(2)]
         taps_sb = keep.tile([P, PACK, 3], F32, name="taps_sb")
 
         nc.gpsimd.memset(scale_table[:].bitcast(I32), 0)
-        def load_w1(o):
-            nc.sync.dma_start(
-                out=w1_raw[o][:], in_=w1[o * K_PASS : (o + 1) * K_PASS, :].rearrange("(p j) c -> p j c", j=PACK)
-            )
+        w1_rows = w1.rearrange("(o p j) c -> o p j c", o=PASSES, j=PACK)
 
-        def load_scales(o, q):
-            row = 32 * q + 4 * o
+        def load_scales(q):
             nc.sync.dma_start(
-                out=scale_table[row : row + 4, :].bitcast(I32), in_=x_scales[o, 4 * q : 4 * q + 4, :].bitcast(I32)
+                out=scale_table[32 * q : 32 * q + 8, :].bitcast(I32), in_=x_scales[:, 4 * q : 4 * q + 4, :].bitcast(I32)
             )
 
         def load_words(o):
@@ -80,16 +90,15 @@ def tile_picked_yserial_none_po_kernel(
                 out=word_table[o][:].bitcast(I32), in_=x_words[o].rearrange("p c r -> p (c r)").bitcast(I32)
             )
 
-        load_w1(0)
-        for q in range(4):
-            load_scales(0, q)
+        nc.sync.dma_start(out=w1_first[:], in_=w1_rows[0])
+        for q in (0, 2, 1, 3):
+            load_scales(q)
         nc.sync.dma_start(out=offs_sb[:], in_=offs)
         load_words(0)
-        nc.sync.dma_start(out=taps_sb[:], in_=taps.rearrange("(p t) e -> p t e", t=PACK))
-        for q in range(4):
-            load_scales(1, q)
-        load_w1(1)
         load_words(1)
+        for h in range(2):
+            nc.sync.dma_start(out=w1_last[h][:], in_=w1_rows[1][:, :, h * 256 : (h + 1) * 256])
+        nc.sync.dma_start(out=taps_sb[:], in_=taps.rearrange("(p t) e -> p t e", t=PACK))
         w2_rows = w2.rearrange("(p j) c -> p j c", j=PACK)
         nc.sync.dma_start(out=w2_raw[0][:], in_=w2_rows[:, :, 0:256])
         nc.sync.dma_start(out=order_sb[:], in_=order)
@@ -106,35 +115,45 @@ def tile_picked_yserial_none_po_kernel(
         w1_code = [keep.tile([P, H], U32, name="w1_code%d" % o, align_bytes=64) for o in range(PASSES)]
         w1_scale = [keep.tile([P, H], U8, name="w1_scale%d" % o, align_bytes=64) for o in range(PASSES)]
         w1_bf = [keep.tile([P, PACK * H], BF16, name="w1_bf%d" % o, tag="w1_bf%d" % o, align_bytes=64) for o in range(PASSES)]
-        y_parts = [(0, 0, 256), (0, 256, 512), (1, 0, 512), (2, 0, 512), (3, 0, 512)]
+        y_parts = [(0, a, b) for a, b in X_CUTS] + [(t, 0, S) for t in range(1, PACK)]
         y_ps = [psum.tile([P, b - a], F32, name="y_ps%d" % n, tag="y_ps%d" % n) for n, (t, a, b) in enumerate(y_parts)]
         w2_bf = keep.tile([P, PACK * N], BF16, name="w2_bf", align_bytes=64)
 
         x_scale = keep.tile([P, S], U8, name="x_scale", align_bytes=64)
-        for o in range(PASSES):
-            deal(nc.vector.tensor_copy, w1_bf[o], w1_raw[o], 0, W1_SPLIT)
-            deal(scalar_cast(nc), w1_bf[o], w1_raw[o], W1_SPLIT, P)
-            nc.vector.quantize_mx(out=w1_code[o][:].bitcast(FP8X4), scales=w1_scale[o][:], in_=w1_bf[o][:])
-            if o == 0:
-                nc.vector.tensor_copy(out=x_code[o][:], in_=word_table[o][:].indirect(offs_sb[:]))
-                nc.vector.tensor_copy(out=x_scale[:], in_=scale_table[:].indirect(offs_sb[:]))
-            else:
-                for h in range(2):
-                    nc.vector.tensor_copy(
-                        out=x_code[o][:, h * 256 : (h + 1) * 256],
-                        in_=word_table[o][:].indirect(offs_sb[:, h * 16 : (h + 1) * 16]),
+        def first_product(o, t):
+            cols = slice(t * P, (t + 1) * P)
+            for n, (owner, a, b) in enumerate(y_parts):
+                if owner == t:
+                    nc.tensor.matmul_mx(
+                        out=y_ps[n][:],
+                        lhsT=w1_code[o][:, cols].bitcast(FP8X4),
+                        lhsT_scale=w1_scale[o][:, cols],
+                        rhs=x_code[o][:, a:b].bitcast(FP8X4),
+                        rhs_scale=x_scale[4 * o : P, a:b],
+                        start=(o == 0),
+                        stop=(o == PASSES - 1),
                     )
-            for n, (t, a, b) in enumerate(y_parts):
-                cols = slice(t * P, (t + 1) * P)
-                nc.tensor.matmul_mx(
-                    out=y_ps[n][:],
-                    lhsT=w1_code[o][:, cols].bitcast(FP8X4),
-                    lhsT_scale=w1_scale[o][:, cols],
-                    rhs=x_code[o][:, a:b].bitcast(FP8X4),
-                    rhs_scale=x_scale[4 * o : P, a:b],
-                    start=(o == 0),
-                    stop=(o == PASSES - 1),
-                )
+
+        deal(nc.vector.tensor_copy, w1_bf[0], w1_first, 0, W1_SPLIT)
+        deal(scalar_cast(nc), w1_bf[0], w1_first, W1_SPLIT, P)
+        nc.vector.quantize_mx(out=w1_code[0][:].bitcast(FP8X4), scales=w1_scale[0][:], in_=w1_bf[0][:])
+        nc.vector.tensor_copy(out=x_scale[:], in_=scale_table[:].indirect(offs_sb[:]))
+        nc.vector.tensor_copy(out=x_code[0][:], in_=word_table[0][:].indirect(offs_sb[:]))
+        for t in range(PACK):
+            first_product(0, t)
+        nc.vector.tensor_copy(out=x_code[1][:], in_=word_table[1][:].indirect(offs_sb[:]))
+        for h in range(2):
+            m0, cut = 64 * h, 64 * h + HALF_SPLITS[h]
+            deal(nc.vector.tensor_copy, w1_bf[1], w1_last[h], m0, cut, base=m0)
+            deal(scalar_cast(nc), w1_bf[1], w1_last[h], cut, m0 + 64, base=m0)
+        for t in range(PACK):
+            cols = slice(t * P, (t + 1) * P)
+            nc.vector.quantize_mx(
+                out=w1_code[1][:, cols].bitcast(FP8X4),
+                scales=w1_scale[1][:, cols],
+                in_=w1_bf[1][:, t * K_PASS : (t + 1) * K_PASS],
+            )
+            first_product(1, t)
 
         keep_gain = keep.tile([P, PACK], F32, name="keep_gain")
         nc.scalar.activation(out=keep_gain[:], in_=taps_sb[:, :, 0], func=COPY, bias=1.0)
@@ -174,79 +193,108 @@ def tile_picked_yserial_none_po_kernel(
         keep_own(3)
         deal(nc.scalar.copy, w2_bf, w2_raw[1], 64, 128, base=64)
 
-        z = [keep.tile([P, PACK, b - a], F32, name="z%d" % a, align_bytes=64)[:] for a, b in PIECES[:2]]
-        shared = keep.tile([P, 768], F32, name="shared", align_bytes=64)
-        last_bf = keep.tile([P, 512], BF16, name="last_bf", tag="late", align_bytes=64)
-        z_bf = [shared[:, 0:512].bitcast(BF16), shared[:, 512:768].bitcast(BF16), last_bf[:]]
-        z.append(shared[:, 256:768].rearrange("p (t c) -> p t c", t=PACK))
+        z_bf = keep.tile([P, PACK * S], BF16, name="z_bf", align_bytes=64)
         z_code = [keep.tile([P, b - a], U32, name="z_code%d" % a, align_bytes=64) for a, b in PIECES]
         z_scale = [keep.tile([P, b - a], U8, name="z_scale%d" % a, align_bytes=64) for a, b in PIECES]
-        res = [keep.tile([P, PACK, b - a], F32, name="res%d" % a, align_bytes=64) for a, b in PIECES]
-        res_code = [keep.tile([P, b - a], U32, name="res_code%d" % a, align_bytes=64) for a, b in PIECES]
+        res = [keep.tile([P, PACK, b - a], F32, name="res%d" % a, align_bytes=64) for a, b in STORES]
+        res_bf = keep.tile([P, PACK * S], BF16, name="res_bf", align_bytes=64)
+        res_code = keep.tile([P, S], U32, name="res_code", align_bytes=64)
         res_scale = keep.tile([P, S], U8, name="res_scale", align_bytes=64)
         out_rows = out_0.rearrange("(p t) j -> p t j", t=PACK)
         out_words = out_1[0].rearrange("p c r -> p (c r)").bitcast(I32)
+        z = {}
+        bank = {}
+        free_banks = ["res_ps0", "res_ps1", "res_ps2"] + ["y_ps%d" % n for n in range(len(y_parts))]
 
         def bring_back(i, t):
-            a, b = PIECES[i]
+            a, b = GROUPS[i]
+            if t == 0:
+                z[i] = keep.tile([P, PACK, b - a], F32, name="z%d" % i, tag="z", bufs=2, align_bytes=64)
             nc.vector.tensor_tensor(
                 out=z[i][:, t, :], in0=rr[t][:].indirect(back_sb[:, a // 16 : b // 16]), in1=y_kept[t][:, a:b], op=ADD
             )
 
-        def round_z(i):
-            weave(nc.vector.tensor_copy if i == 2 else nc.scalar.copy, z_bf[i], z[i])
+        def round_z(i, engine_copy):
+            a, b = GROUPS[i]
+            weave_by_lines(engine_copy, z_bf[:, PACK * a : PACK * b], z[i][:])
 
         def second_product(i):
             a, b = PIECES[i]
-            width = b - a
-            nc.vector.quantize_mx(out=z_code[i][:].bitcast(FP8X4), scales=z_scale[i][:], in_=z_bf[i])
-            per_bank = 4 if i == 1 else 2
-            for t0 in range(0, PACK, per_bank):
-                tag = "y_ps%d" % (t0 // 2) if i == 2 else "res_ps%d_%d" % (a, t0)
-                bank = psum.tile([P, per_bank, width], F32, name="res_ps%d_%d" % (a, t0), tag=tag)
-                for t in range(t0, t0 + per_bank):
-                    cols = slice(t * P, (t + 1) * P)
-                    nc.tensor.matmul_mx(
-                        out=bank[:, t - t0, :],
-                        lhsT=w2_code[:, cols].bitcast(FP8X4),
-                        lhsT_scale=w2_scale[:, cols],
-                        rhs=z_code[i][:].bitcast(FP8X4),
-                        rhs_scale=z_scale[i][:],
-                        start=True,
-                        stop=True,
-                    )
-                nc.scalar.copy(out=res[i][:, t0 : t0 + per_bank, :], in_=bank[:])
-            nc.sync.dma_start(out=out_rows[:, :, a:b], in_=res[i][:])
+            nc.vector.quantize_mx(out=z_code[i][:].bitcast(FP8X4), scales=z_scale[i][:], in_=z_bf[:, PACK * a : PACK * b])
+            per_bank = min(PACK, 512 // (b - a))
+            bank[i] = []
+            for t in range(PACK):
+                if t % per_bank == 0:
+                    tag = free_banks.pop(0)
+                    bank[i].append(psum.tile([P, per_bank, b - a], F32, name="res_ps%d_%d" % (i, t), tag=tag))
+                cols = slice(t * P, (t + 1) * P)
+                nc.tensor.matmul_mx(
+                    out=bank[i][-1][:, t % per_bank, :],
+                    lhsT=w2_code[:, cols].bitcast(FP8X4),
+                    lhsT_scale=w2_scale[:, cols],
+                    rhs=z_code[i][:].bitcast(FP8X4),
+                    rhs_scale=z_scale[i][:],
+                    start=True,
+                    stop=True,
+                )
 
-        def hand_on(i):
+        def in_sbuf(i):
             a, b = PIECES[i]
-            tag = "late" if i == 0 else "res_bf%d" % a
-            res_bf = keep.tile([P, PACK * (b - a)], BF16, name="res_bf%d" % a, tag=tag, align_bytes=64)
-            weave(nc.scalar.copy if i == 1 else nc.vector.tensor_copy, res_bf[:], res[i][:])
-            nc.vector.quantize_mx(out=res_code[i][:].bitcast(FP8X4), scales=res_scale[:, a:b], in_=res_bf[:])
-            nc.sync.dma_start(out=out_words[:, a:b], in_=res_code[i][:].bitcast(I32))
+            n = [s0 <= a < s1 for s0, s1 in STORES].index(True)
+            return n, res[n][:, :, a - STORES[n][0] : b - STORES[n][0]]
+
+        def round_res(i, engine_copy):
+            a, b = PIECES[i]
+            weave(engine_copy, res_bf[:, PACK * a : PACK * b], bank[i][0][:])
+
+        def round_stored(i, engine_copy):
+            a, b = PIECES[i]
+            weave_by_lines(engine_copy, res_bf[:, PACK * a : PACK * b], in_sbuf(i)[1])
+
+        def store_res(i):
+            n, place = in_sbuf(i)
+            per_bank = PACK // len(bank[i])
+            for k, part in enumerate(bank[i]):
+                nc.scalar.copy(out=place[:, k * per_bank : (k + 1) * per_bank, :], in_=part[:])
+            a, b = STORES[n]
+            if b == PIECES[i][1]:
+                nc.sync.dma_start(out=out_rows[:, :, a:b], in_=res[n][:])
+
+        def hand_on(h):
+            a, b = HANDED[h]
+            nc.vector.quantize_mx(
+                out=res_code[:, a:b].bitcast(FP8X4), scales=res_scale[:, a:b], in_=res_bf[:, PACK * a : PACK * b]
+            )
+            for c0, c1 in CODE_STORES:
+                if c1 == b:
+                    nc.sync.dma_start(out=out_words[:, c0:c1], in_=res_code[:, c0:c1].bitcast(I32))
 
         bring_back(0, 0)
         filter_sum(PACK - 1)
         for t in range(1, PACK):
             bring_back(0, t)
-        round_z(0)
+        round_z(0, nc.scalar.copy)
         nc.vector.quantize_mx(out=w2_code[:].bitcast(FP8X4), scales=w2_scale[:], in_=w2_bf[:])
-        for t in range(PACK):
-            bring_back(1, t)
-        round_z(1)
-        second_product(0)
-        bring_back(2, 0)
-        bring_back(2, 1)
-        second_product(1)
-        bring_back(2, 2)
-        bring_back(2, 3)
-        round_z(2)
-        second_product(2)
-        for i in range(len(PIECES)):
-            hand_on(i)
+        last = len(PIECES) - 1
+        for i in range(1, last + 1):
+            for t in range(PACK):
+                bring_back(i, t)
+            second_product(i - 1)
+            round_z(i, nc.scalar.copy if i < last else nc.vector.tensor_copy)
+            if i > 1:
+                store_res(i - 2)
+        second_product(last)
+        for i in range(last - 2):
+            round_res(i, nc.scalar.copy)
+        round_stored(last - 2, nc.vector.tensor_copy)
+        hand_on(0)
+        store_res(last - 1)
+        round_res(last - 1, nc.scalar.copy)
+        round_res(last, nc.vector.tensor_copy)
+        store_res(last)
+        hand_on(1)
         for q in range(4):
-            queue = nc.scalar if q % 2 else nc.sync
+            queue = nc.sync if q % 2 else nc.scalar
             queue.dma_start(
                 out=out_2[0, 4 * q : 4 * q + 4, :].bitcast(I32), in_=res_scale[32 * q : 32 * q + 4, :].bitcast(I32)
             )

@@ -29,13 +29,13 @@ CODE_STORES = ((0, 512),)
 GROUPS = PIECES
 X_CUTS = ((0, 256), (256, 512))
 W1_SPLIT = 72
-HALF_SPLITS = (24, 40)
+LAST_PARTS = ((0, 64, 96), (96, 116, 128))
 
 
 def deal(engine_copy, grouped, raw, m0, m1, base=0):
     engine_copy(
-        out=grouped[:].rearrange("p (t m j) -> p m t j", t=PACK, j=PACK)[:, m0:m1],
-        in_=raw[:].rearrange("p j (m t) -> p m t j", t=PACK)[:, m0 - base : m1 - base],
+        out=grouped[:].rearrange("p (t m j) -> p m j t", t=PACK, j=PACK)[:, m0:m1],
+        in_=raw[:].rearrange("p j (m t) -> p m j t", t=PACK)[:, m0 - base : m1 - base],
     )
 
 
@@ -73,7 +73,7 @@ def tile_picked_yserial_none_po_kernel(
         scale_table = keep.tile([P, T], U8, name="scale_table", align_bytes=64)
         word_table = [keep.tile([P, T], U32, name="word_table%d" % o, align_bytes=64) for o in range(PASSES)]
         w1_first = keep.tile([P, PACK, H], F32, name="w1_first", align_bytes=64)
-        w1_last = [keep.tile([P, PACK, H // 2], F32, name="w1_last%d" % h, align_bytes=64) for h in range(2)]
+        w1_last = [keep.tile([P, PACK, PACK * (m1 - m0)], F32, name="w1_last%d" % m0, align_bytes=64) for m0, cut, m1 in LAST_PARTS]
         w2_raw = [keep.tile([P, PACK, N // 2], F32, name="w2_raw%d" % h, align_bytes=64) for h in range(2)]
         taps_sb = keep.tile([P, PACK, 3], F32, name="taps_sb")
 
@@ -96,8 +96,8 @@ def tile_picked_yserial_none_po_kernel(
         nc.sync.dma_start(out=offs_sb[:], in_=offs)
         load_words(0)
         load_words(1)
-        for h in range(2):
-            nc.sync.dma_start(out=w1_last[h][:], in_=w1_rows[1][:, :, h * 256 : (h + 1) * 256])
+        for h, (m0, cut, m1) in enumerate(LAST_PARTS):
+            nc.sync.dma_start(out=w1_last[h][:], in_=w1_rows[1][:, :, PACK * m0 : PACK * m1])
         nc.sync.dma_start(out=taps_sb[:], in_=taps.rearrange("(p t) e -> p t e", t=PACK))
         w2_rows = w2.rearrange("(p j) c -> p j c", j=PACK)
         nc.sync.dma_start(out=w2_raw[0][:], in_=w2_rows[:, :, 0:256])
@@ -142,10 +142,9 @@ def tile_picked_yserial_none_po_kernel(
         for t in range(PACK):
             first_product(0, t)
         nc.vector.tensor_copy(out=x_code[1][:], in_=word_table[1][:].indirect(offs_sb[:]))
-        for h in range(2):
-            m0, cut = 64 * h, 64 * h + HALF_SPLITS[h]
+        for h, (m0, cut, m1) in enumerate(LAST_PARTS):
             deal(nc.vector.tensor_copy, w1_bf[1], w1_last[h], m0, cut, base=m0)
-            deal(scalar_cast(nc), w1_bf[1], w1_last[h], cut, m0 + 64, base=m0)
+            deal(scalar_cast(nc), w1_bf[1], w1_last[h], cut, m1, base=m0)
         for t in range(PACK):
             cols = slice(t * P, (t + 1) * P)
             nc.vector.quantize_mx(
@@ -276,10 +275,12 @@ def tile_picked_yserial_none_po_kernel(
         round_z(0, nc.scalar.copy)
         nc.vector.quantize_mx(out=w2_code[:].bitcast(FP8X4), scales=w2_scale[:], in_=w2_bf[:])
         last = len(PIECES) - 1
+        second_product(0)
         for i in range(1, last + 1):
             for t in range(PACK):
                 bring_back(i, t)
-            second_product(i - 1)
+            if i > 1:
+                second_product(i - 1)
             round_z(i, nc.scalar.copy if i < last else nc.vector.tensor_copy)
             if i > 1:
                 store_res(i - 2)

@@ -20,13 +20,10 @@ P = 128
 PACK = 4
 K_PASS = P * PACK
 PASSES = K // K_PASS
-Y_WINDOW = 704
+Y_WINDOW = 528
 LEAD = 4
-PIECES = ((0, 64), (64, 192), (192, 320), (320, 448), (448, 512))
-STORES = PIECES
-HANDED = ((0, 256), (256, 512))
-CODE_STORES = ((0, 512),)
-GROUPS = PIECES
+PIECES = ((0, 128), (128, 256), (256, 384), (384, 512))
+HALVES = ((0, 256), (256, 512))
 X_CUTS = ((0, 256), (256, 512))
 W1_SPLIT = 72
 LAST_PARTS = ((0, 64, 96), (96, 116, 128))
@@ -105,10 +102,11 @@ def tile_picked_yserial_none_po_kernel(
         nc.sync.dma_start(out=back_sb[:], in_=back)
         nc.sync.dma_start(out=w2_raw[1][:], in_=w2_rows[:, :, 256:512])
 
-        y = [keep.tile([P, Y_WINDOW], F32, name="y%d" % t, align_bytes=64) for t in range(PACK)]
+        y = [keep.tile([P, Y_WINDOW if t else S], F32, name="y%d" % t, align_bytes=64) for t in range(PACK)]
         gg = [keep.tile([P, LEAD + S], F32, name="gg%d" % t, align_bytes=64) for t in range(PACK)]
         for t in range(PACK):
-            nc.vector.memset(y[t][:, S:Y_WINDOW], 0.0)
+            if t:
+                nc.vector.memset(y[t][:, S:Y_WINDOW], 0.0)
             nc.vector.memset(gg[t][:, 0:LEAD], 0.0)
 
         x_code = [keep.tile([P, S], U32, name="x_code%d" % o, align_bytes=64) for o in range(PASSES)]
@@ -154,81 +152,78 @@ def tile_picked_yserial_none_po_kernel(
             )
             first_product(1, t)
 
-        keep_gain = keep.tile([P, PACK], F32, name="keep_gain")
-        nc.scalar.activation(out=keep_gain[:], in_=taps_sb[:, :, 0], func=COPY, bias=1.0)
+        gain = keep.tile([P, PACK], F32, name="gain")
+        nc.scalar.activation(out=gain[:], in_=taps_sb[:, :, 0], func=COPY, bias=1.0)
 
-        y_kept = [keep.tile([P, S], F32, name="y_kept%d" % t, align_bytes=64) for t in range(PACK)]
         far = [keep.tile([P, S], F32, name="far%d" % t, align_bytes=64) for t in range(PACK)]
+        near = [keep.tile([P, S], F32, name="near%d" % t, align_bytes=64) for t in range(PACK)]
         rr = [keep.tile([P, S], F32, name="rr%d" % t, align_bytes=64) for t in range(PACK)]
         w2_code = keep.tile([P, N], U32, name="w2_code", align_bytes=64)
         w2_scale = keep.tile([P, N], U8, name="w2_scale", align_bytes=64)
 
-        def filter_sum(t):
+        def vector_gather(out, window, offsets):
+            nc.vector.tensor_copy(out=out, in_=window.indirect(offsets))
+
+        def scalar_gather(out, window, offsets):
+            nc.scalar.activation(out=out, in_=window.indirect(offsets), func=COPY)
+
+        def leave_psum(n, engine_copy):
+            t, a, b = y_parts[n]
+            engine_copy(out=y[t][:, a:b], in_=y_ps[n][:])
+
+        def by_order(gather, t, a, b):
+            gather(gg[t][:, LEAD + a : LEAD + b], y[t][:], order_sb[:, a // 16 : b // 16])
+
+        def far_tap(t):
+            nc.vector.tensor_scalar(
+                out=far[t][:], in0=gg[t][:, LEAD - 2 : LEAD - 2 + S], scalar1=taps_sb[:, t, 2:3], scalar2=None, op0=MULT
+            )
+
+        def near_tap(t):
             nc.vector.scalar_tensor_tensor(
-                out=rr[t][:], in0=gg[t][:, LEAD - 1 : LEAD - 1 + S], scalar=taps_sb[:, t, 1:2], in1=far[t][:],
+                out=near[t][:], in0=gg[t][:, LEAD - 1 : LEAD - 1 + S], scalar=taps_sb[:, t, 1:2], in1=far[t][:],
                 op0=MULT, op1=ADD,
             )
 
-        deal(nc.vector.tensor_copy, w2_bf, w2_raw[0], 0, 64)
-        for n, (t, a, b) in enumerate(y_parts):
-            nc.scalar.copy(out=y[t][:, a:b], in_=y_ps[n][:])
-        def keep_own(t):
-            for n, (owner, a, b) in enumerate(y_parts):
-                if owner == t:
-                    nc.scalar.activation(
-                        out=y_kept[t][:, a:b], in_=y_ps[n][:], func=COPY, scale=keep_gain[:, t : t + 1]
-                    )
-
-        for t in range(PACK):
-            nc.vector.tensor_copy(out=gg[t][:, LEAD : LEAD + S], in_=y[t][:].indirect(order_sb[:]))
-            nc.scalar.activation(
-                out=far[t][:], in_=gg[t][:, LEAD - 2 : LEAD - 2 + S], func=COPY, scale=taps_sb[:, t, 2:3]
+        def own_tap(t):
+            nc.vector.scalar_tensor_tensor(
+                out=rr[t][:], in0=gg[t][:, LEAD : LEAD + S], scalar=gain[:, t : t + 1], in1=near[t][:],
+                op0=MULT, op1=ADD,
             )
-            if t in (1, 2):
-                keep_own(t - 1)
-            if t > 0:
-                filter_sum(t - 1)
-        keep_own(2)
-        keep_own(3)
-        deal(nc.scalar.copy, w2_bf, w2_raw[1], 64, 128, base=64)
 
+        def deal_w2(n):
+            deal(nc.vector.tensor_copy, w2_bf, w2_raw[n // 2], 32 * n, 32 * n + 32, base=64 * (n // 2))
+
+        z = [keep.tile([P, PACK, b - a], BF16, name="z%d" % a, align_bytes=64) for a, b in HALVES]
         z_bf = keep.tile([P, PACK * S], BF16, name="z_bf", align_bytes=64)
         z_code = [keep.tile([P, b - a], U32, name="z_code%d" % a, align_bytes=64) for a, b in PIECES]
         z_scale = [keep.tile([P, b - a], U8, name="z_scale%d" % a, align_bytes=64) for a, b in PIECES]
-        res = [keep.tile([P, PACK, b - a], F32, name="res%d" % a, align_bytes=64) for a, b in STORES]
+        res = [keep.tile([P, PACK, b - a], F32, name="res%d" % a, align_bytes=64) for a, b in PIECES]
         res_bf = keep.tile([P, PACK * S], BF16, name="res_bf", align_bytes=64)
         res_code = keep.tile([P, S], U32, name="res_code", align_bytes=64)
         res_scale = keep.tile([P, S], U8, name="res_scale", align_bytes=64)
         out_rows = out_0.rearrange("(p t) j -> p t j", t=PACK)
         out_words = out_1[0].rearrange("p c r -> p (c r)").bitcast(I32)
-        z = {}
-        bank = {}
-        free_banks = ["res_ps0", "res_ps1", "res_ps2"] + ["y_ps%d" % n for n in range(len(y_parts))]
+        bank = [psum.tile([P, PACK, b - a], F32, name="res_ps%d" % i, tag="res_ps%d" % i if i < 3 else "y_ps0") for i, (a, b) in enumerate(PIECES)]
 
-        def bring_back(i, t):
-            a, b = GROUPS[i]
-            if t == 0:
-                z[i] = keep.tile([P, PACK, b - a], F32, name="z%d" % i, tag="z", bufs=2, align_bytes=64)
-            nc.vector.tensor_tensor(
-                out=z[i][:, t, :], in0=rr[t][:].indirect(back_sb[:, a // 16 : b // 16]), in1=y_kept[t][:, a:b], op=ADD
-            )
+        def z_part(a, b):
+            h = a // 256
+            return z[h][:, :, a - 256 * h : b - 256 * h]
 
-        def round_z(i, engine_copy):
-            a, b = GROUPS[i]
-            weave_by_lines(engine_copy, z_bf[:, PACK * a : PACK * b], z[i][:])
+        def by_back(gather, t, a, b):
+            gather(z_part(a, b)[:, t, :], rr[t][:], back_sb[:, a // 16 : b // 16])
+
+        def weave_z(i, engine_copy):
+            a, b = PIECES[i]
+            weave_by_lines(engine_copy, z_bf[:, PACK * a : PACK * b], z_part(a, b))
 
         def second_product(i):
             a, b = PIECES[i]
             nc.vector.quantize_mx(out=z_code[i][:].bitcast(FP8X4), scales=z_scale[i][:], in_=z_bf[:, PACK * a : PACK * b])
-            per_bank = min(PACK, 512 // (b - a))
-            bank[i] = []
             for t in range(PACK):
-                if t % per_bank == 0:
-                    tag = free_banks.pop(0)
-                    bank[i].append(psum.tile([P, per_bank, b - a], F32, name="res_ps%d_%d" % (i, t), tag=tag))
                 cols = slice(t * P, (t + 1) * P)
                 nc.tensor.matmul_mx(
-                    out=bank[i][-1][:, t % per_bank, :],
+                    out=bank[i][:, t, :],
                     lhsT=w2_code[:, cols].bitcast(FP8X4),
                     lhsT_scale=w2_scale[:, cols],
                     rhs=z_code[i][:].bitcast(FP8X4),
@@ -237,63 +232,77 @@ def tile_picked_yserial_none_po_kernel(
                     stop=True,
                 )
 
-        def in_sbuf(i):
+        def round_bank(i, engine_copy):
             a, b = PIECES[i]
-            n = [s0 <= a < s1 for s0, s1 in STORES].index(True)
-            return n, res[n][:, :, a - STORES[n][0] : b - STORES[n][0]]
-
-        def round_res(i, engine_copy):
-            a, b = PIECES[i]
-            weave(engine_copy, res_bf[:, PACK * a : PACK * b], bank[i][0][:])
+            weave(engine_copy, res_bf[:, PACK * a : PACK * b], bank[i][:])
 
         def round_stored(i, engine_copy):
             a, b = PIECES[i]
-            weave_by_lines(engine_copy, res_bf[:, PACK * a : PACK * b], in_sbuf(i)[1])
+            weave_by_lines(engine_copy, res_bf[:, PACK * a : PACK * b], res[i][:])
 
         def store_res(i):
-            n, place = in_sbuf(i)
-            per_bank = PACK // len(bank[i])
-            for k, part in enumerate(bank[i]):
-                nc.scalar.copy(out=place[:, k * per_bank : (k + 1) * per_bank, :], in_=part[:])
-            a, b = STORES[n]
-            if b == PIECES[i][1]:
-                nc.sync.dma_start(out=out_rows[:, :, a:b], in_=res[n][:])
+            a, b = PIECES[i]
+            nc.scalar.copy(out=res[i][:], in_=bank[i][:])
+            nc.sync.dma_start(out=out_rows[:, :, a:b], in_=res[i][:])
 
         def hand_on(h):
-            a, b = HANDED[h]
+            a, b = HALVES[h]
             nc.vector.quantize_mx(
                 out=res_code[:, a:b].bitcast(FP8X4), scales=res_scale[:, a:b], in_=res_bf[:, PACK * a : PACK * b]
             )
-            for c0, c1 in CODE_STORES:
-                if c1 == b:
-                    nc.sync.dma_start(out=out_words[:, c0:c1], in_=res_code[:, c0:c1].bitcast(I32))
 
-        bring_back(0, 0)
-        filter_sum(PACK - 1)
+        leave_psum(0, nc.vector.tensor_copy)
+        leave_psum(1, nc.scalar.copy)
+        by_order(vector_gather, 0, 0, 256)
+        by_order(scalar_gather, 0, 256, 512)
         for t in range(1, PACK):
-            bring_back(0, t)
-        round_z(0, nc.scalar.copy)
+            leave_psum(t + 1, nc.scalar.copy)
+            by_order(scalar_gather, t, 0, S)
+        deal_w2(0)
+        far_tap(0)
+        deal_w2(1)
+        near_tap(0)
+        deal_w2(2)
+        own_tap(0)
+        far_tap(1)
+        deal_w2(3)
+        near_tap(1)
+        far_tap(2)
+        own_tap(1)
+        near_tap(2)
+        far_tap(3)
+        own_tap(2)
+        near_tap(3)
         nc.vector.quantize_mx(out=w2_code[:].bitcast(FP8X4), scales=w2_scale[:], in_=w2_bf[:])
-        last = len(PIECES) - 1
+        own_tap(3)
+        for t in range(3):
+            by_back(scalar_gather, t, 0, 256)
+        for t in range(2):
+            by_back(scalar_gather, t, 256, 512)
+        by_back(vector_gather, 3, 0, 128)
+        by_back(scalar_gather, 3, 128, 256)
+        by_back(scalar_gather, 2, 256, 512)
+        by_back(scalar_gather, 3, 256, 384)
+        by_back(scalar_gather, 3, 384, 512)
+        weave_z(0, nc.vector.tensor_copy)
+        weave_z(1, nc.vector.tensor_copy)
         second_product(0)
-        for i in range(1, last + 1):
-            for t in range(PACK):
-                bring_back(i, t)
-            if i > 1:
-                second_product(i - 1)
-            round_z(i, nc.scalar.copy if i < last else nc.vector.tensor_copy)
-            if i > 1:
-                store_res(i - 2)
-        second_product(last)
-        for i in range(last - 2):
-            round_res(i, nc.scalar.copy)
-        round_stored(last - 2, nc.vector.tensor_copy)
+        second_product(1)
+        weave_z(2, nc.vector.tensor_copy)
+        weave_z(3, nc.vector.tensor_copy)
+        second_product(2)
+        second_product(3)
+        store_res(0)
+        round_stored(0, nc.vector.tensor_copy)
+        store_res(1)
+        round_stored(1, nc.vector.tensor_copy)
+        store_res(2)
         hand_on(0)
-        store_res(last - 1)
-        round_res(last - 1, nc.scalar.copy)
-        round_res(last, nc.vector.tensor_copy)
-        store_res(last)
+        round_stored(2, nc.vector.tensor_copy)
+        round_bank(3, nc.vector.tensor_copy)
+        store_res(3)
         hand_on(1)
+        nc.sync.dma_start(out=out_words, in_=res_code[:].bitcast(I32))
         for q in range(4):
             queue = nc.sync if q % 2 else nc.scalar
             queue.dma_start(

@@ -24,9 +24,8 @@ Y_WINDOW = 528
 LEAD = 4
 PIECES = ((0, 128), (128, 256), (256, 384), (384, 512))
 HALVES = ((0, 256), (256, 512))
-X_CUTS = ((0, 256), (256, 512))
-W1_SPLIT = 72
-LAST_PARTS = ((0, 64, 96), (96, 116, 128))
+X_CUTS = ((0, 256), (256, 384), (384, 512))
+W1_SPLIT = (32, 64)
 
 
 def deal(engine_copy, grouped, raw, m0, m1, base=0):
@@ -67,40 +66,41 @@ def tile_picked_yserial_none_po_kernel(
         order_sb = lists.tile([P, S // 16], U16, name="order_sb")
         back_sb = lists.tile([P, S // 16], U16, name="back_sb")
 
-        scale_table = keep.tile([P, T], U8, name="scale_table", align_bytes=64)
-        word_table = [keep.tile([P, T], U32, name="word_table%d" % o, align_bytes=64) for o in range(PASSES)]
-        w1_first = keep.tile([P, PACK, H], F32, name="w1_first", align_bytes=64)
-        w1_last = [keep.tile([P, PACK, PACK * (m1 - m0)], F32, name="w1_last%d" % m0, align_bytes=64) for m0, cut, m1 in LAST_PARTS]
-        w2_raw = [keep.tile([P, PACK, N // 2], F32, name="w2_raw%d" % h, align_bytes=64) for h in range(2)]
+        scale_table = keep.tile([P, T], U8, name="scale_table", tag="table1", align_bytes=64)
+        word_table = [keep.tile([P, T], U32, name="word_table%d" % o, tag="table%d" % o, align_bytes=64) for o in range(PASSES)]
+        w1_raw = [keep.tile([P, PACK, H], F32, name="w1_raw%d" % o, tag="raw%d" % o, align_bytes=64) for o in range(PASSES)]
+        w2_raw = keep.tile([P, PACK, N], F32, name="w2_raw", tag="raw0", align_bytes=64)
         taps_sb = keep.tile([P, PACK, 3], F32, name="taps_sb")
+        picked = keep.tile([P, S], U8, name="picked", align_bytes=64)
+        x_scale = keep.tile([P, PASSES, S], U8, name="x_scale", align_bytes=64)
 
-        nc.gpsimd.memset(scale_table[:].bitcast(I32), 0)
+        nc.vector.memset(scale_table[:, 0 : T // 2].bitcast(I32), 0)
+        nc.gpsimd.memset(scale_table[:, T // 2 : T].bitcast(I32), 0)
+        nc.gpsimd.memset(x_scale[:].bitcast(I32), 0)
         w1_rows = w1.rearrange("(o p j) c -> o p j c", o=PASSES, j=PACK)
-
-        def load_scales(q):
-            nc.sync.dma_start(
-                out=scale_table[32 * q : 32 * q + 8, :].bitcast(I32), in_=x_scales[:, 4 * q : 4 * q + 4, :].bitcast(I32)
-            )
 
         def load_words(o):
             nc.sync.dma_start(
                 out=word_table[o][:].bitcast(I32), in_=x_words[o].rearrange("p c r -> p (c r)").bitcast(I32)
             )
 
-        nc.sync.dma_start(out=w1_first[:], in_=w1_rows[0])
-        for q in (0, 2, 1, 3):
-            load_scales(q)
+        nc.sync.dma_start(out=w1_raw[0][:], in_=w1_rows[0])
+        for o in range(PASSES):
+            nc.sync.dma_start(out=scale_table[4 * o : P : 8, :].bitcast(I32), in_=x_scales[o].bitcast(I32))
         nc.sync.dma_start(out=offs_sb[:], in_=offs)
+        nc.sync.dma_start(out=w1_raw[1][:], in_=w1_rows[1])
         load_words(0)
-        load_words(1)
-        for h, (m0, cut, m1) in enumerate(LAST_PARTS):
-            nc.sync.dma_start(out=w1_last[h][:], in_=w1_rows[1][:, :, PACK * m0 : PACK * m1])
         nc.sync.dma_start(out=taps_sb[:], in_=taps.rearrange("(p t) e -> p t e", t=PACK))
-        w2_rows = w2.rearrange("(p j) c -> p j c", j=PACK)
-        nc.sync.dma_start(out=w2_raw[0][:], in_=w2_rows[:, :, 0:256])
         nc.sync.dma_start(out=order_sb[:], in_=order)
+        nc.vector.tensor_copy(out=picked[:], in_=scale_table[:].indirect(offs_sb[:]))
+        for q in range(4):
+            nc.sync.dma_start(
+                out=x_scale[32 * q : 32 * q + 4].rearrange("r o c -> r (o c)").bitcast(I32),
+                in_=picked[32 * q : 32 * q + 32 : 4, :].bitcast(I32),
+            )
+        load_words(1)
+        nc.sync.dma_start(out=w2_raw[:], in_=w2.rearrange("(p j) c -> p j c", j=PACK))
         nc.sync.dma_start(out=back_sb[:], in_=back)
-        nc.sync.dma_start(out=w2_raw[1][:], in_=w2_rows[:, :, 256:512])
 
         y = [keep.tile([P, Y_WINDOW if t else S], F32, name="y%d" % t, align_bytes=64) for t in range(PACK)]
         gg = [keep.tile([P, LEAD + S], F32, name="gg%d" % t, align_bytes=64) for t in range(PACK)]
@@ -117,7 +117,6 @@ def tile_picked_yserial_none_po_kernel(
         y_ps = [psum.tile([P, b - a], F32, name="y_ps%d" % n, tag="y_ps%d" % n) for n, (t, a, b) in enumerate(y_parts)]
         w2_bf = keep.tile([P, PACK * N], BF16, name="w2_bf", align_bytes=64)
 
-        x_scale = keep.tile([P, S], U8, name="x_scale", align_bytes=64)
         def first_product(o, t):
             cols = slice(t * P, (t + 1) * P)
             for n, (owner, a, b) in enumerate(y_parts):
@@ -127,29 +126,21 @@ def tile_picked_yserial_none_po_kernel(
                         lhsT=w1_code[o][:, cols].bitcast(FP8X4),
                         lhsT_scale=w1_scale[o][:, cols],
                         rhs=x_code[o][:, a:b].bitcast(FP8X4),
-                        rhs_scale=x_scale[4 * o : P, a:b],
+                        rhs_scale=x_scale[:, o, a:b],
                         start=(o == 0),
                         stop=(o == PASSES - 1),
                     )
 
-        deal(nc.vector.tensor_copy, w1_bf[0], w1_first, 0, W1_SPLIT)
-        deal(scalar_cast(nc), w1_bf[0], w1_first, W1_SPLIT, P)
-        nc.vector.quantize_mx(out=w1_code[0][:].bitcast(FP8X4), scales=w1_scale[0][:], in_=w1_bf[0][:])
-        nc.vector.tensor_copy(out=x_scale[:], in_=scale_table[:].indirect(offs_sb[:]))
+        for o in range(PASSES):
+            deal(nc.vector.tensor_copy, w1_bf[o], w1_raw[o], 0, W1_SPLIT[o])
+            deal(scalar_cast(nc), w1_bf[o], w1_raw[o], W1_SPLIT[o], P)
+            nc.vector.quantize_mx(out=w1_code[o][:].bitcast(FP8X4), scales=w1_scale[o][:], in_=w1_bf[o][:])
         nc.vector.tensor_copy(out=x_code[0][:], in_=word_table[0][:].indirect(offs_sb[:]))
         for t in range(PACK):
             first_product(0, t)
-        nc.vector.tensor_copy(out=x_code[1][:], in_=word_table[1][:].indirect(offs_sb[:]))
-        for h, (m0, cut, m1) in enumerate(LAST_PARTS):
-            deal(nc.vector.tensor_copy, w1_bf[1], w1_last[h], m0, cut, base=m0)
-            deal(scalar_cast(nc), w1_bf[1], w1_last[h], cut, m1, base=m0)
+        for a, b in X_CUTS:
+            nc.vector.tensor_copy(out=x_code[1][:, a:b], in_=word_table[1][:].indirect(offs_sb[:, a // 16 : b // 16]))
         for t in range(PACK):
-            cols = slice(t * P, (t + 1) * P)
-            nc.vector.quantize_mx(
-                out=w1_code[1][:, cols].bitcast(FP8X4),
-                scales=w1_scale[1][:, cols],
-                in_=w1_bf[1][:, t * K_PASS : (t + 1) * K_PASS],
-            )
             first_product(1, t)
 
         gain = keep.tile([P, PACK], F32, name="gain")
@@ -192,7 +183,7 @@ def tile_picked_yserial_none_po_kernel(
             )
 
         def deal_w2(n):
-            deal(nc.vector.tensor_copy, w2_bf, w2_raw[n // 2], 32 * n, 32 * n + 32, base=64 * (n // 2))
+            deal(nc.vector.tensor_copy, w2_bf, w2_raw, 32 * n, 32 * n + 32)
 
         z = [keep.tile([P, PACK, b - a], BF16, name="z%d" % a, align_bytes=64) for a, b in HALVES]
         z_bf = keep.tile([P, PACK * S], BF16, name="z_bf", align_bytes=64)
@@ -204,7 +195,7 @@ def tile_picked_yserial_none_po_kernel(
         res_scale = keep.tile([P, S], U8, name="res_scale", align_bytes=64)
         out_rows = out_0.rearrange("(p t) j -> p t j", t=PACK)
         out_words = out_1[0].rearrange("p c r -> p (c r)").bitcast(I32)
-        bank = [psum.tile([P, PACK, b - a], F32, name="res_ps%d" % i, tag="res_ps%d" % i if i < 3 else "y_ps0") for i, (a, b) in enumerate(PIECES)]
+        bank = [psum.tile([P, PACK, b - a], F32, name="res_ps%d" % i, tag="res_ps%d" % i if i < 2 else "y_ps%d" % (i - 2)) for i, (a, b) in enumerate(PIECES)]
 
         def z_part(a, b):
             h = a // 256
@@ -251,12 +242,13 @@ def tile_picked_yserial_none_po_kernel(
                 out=res_code[:, a:b].bitcast(FP8X4), scales=res_scale[:, a:b], in_=res_bf[:, PACK * a : PACK * b]
             )
 
-        leave_psum(0, nc.vector.tensor_copy)
+        leave_psum(0, nc.scalar.copy)
         leave_psum(1, nc.scalar.copy)
+        leave_psum(2, nc.vector.tensor_copy)
         by_order(vector_gather, 0, 0, 256)
         by_order(scalar_gather, 0, 256, 512)
         for t in range(1, PACK):
-            leave_psum(t + 1, nc.scalar.copy)
+            leave_psum(t + 2, nc.scalar.copy)
             by_order(scalar_gather, t, 0, S)
         deal_w2(0)
         far_tap(0)

@@ -25,7 +25,7 @@ LEAD = 4
 PIECES = ((0, 128), (128, 256), (256, 384), (384, 512))
 HALVES = ((0, 256), (256, 512))
 X_CUTS = ((0, 256), (256, 384), (384, 512))
-W1_SPLIT = (32, 64)
+W1_SPLIT = (32, 80)
 
 
 def deal(engine_copy, grouped, raw, m0, m1, base=0):
@@ -88,8 +88,8 @@ def tile_picked_yserial_none_po_kernel(
         for o in range(PASSES):
             nc.sync.dma_start(out=scale_table[4 * o : P : 8, :].bitcast(I32), in_=x_scales[o].bitcast(I32))
         nc.sync.dma_start(out=offs_sb[:], in_=offs)
-        nc.sync.dma_start(out=w1_raw[1][:], in_=w1_rows[1])
         load_words(0)
+        nc.sync.dma_start(out=w1_raw[1][:], in_=w1_rows[1])
         nc.sync.dma_start(out=taps_sb[:], in_=taps.rearrange("(p t) e -> p t e", t=PACK))
         nc.sync.dma_start(out=order_sb[:], in_=order)
         nc.vector.tensor_copy(out=picked[:], in_=scale_table[:].indirect(offs_sb[:]))
@@ -115,7 +115,7 @@ def tile_picked_yserial_none_po_kernel(
         w1_bf = [keep.tile([P, PACK * H], BF16, name="w1_bf%d" % o, tag="w1_bf%d" % o, align_bytes=64) for o in range(PASSES)]
         y_parts = [(0, a, b) for a, b in X_CUTS] + [(t, 0, S) for t in range(1, PACK)]
         y_ps = [psum.tile([P, b - a], F32, name="y_ps%d" % n, tag="y_ps%d" % n) for n, (t, a, b) in enumerate(y_parts)]
-        w2_bf = keep.tile([P, PACK * N], BF16, name="w2_bf", align_bytes=64)
+        w2_bf = keep.tile([P, PACK * N], BF16, name="w2_bf", tag="w2_bf", align_bytes=64)
 
         def first_product(o, t):
             cols = slice(t * P, (t + 1) * P)
@@ -131,13 +131,16 @@ def tile_picked_yserial_none_po_kernel(
                         stop=(o == PASSES - 1),
                     )
 
-        for o in range(PASSES):
+        def quantise_w1(o):
             deal(nc.vector.tensor_copy, w1_bf[o], w1_raw[o], 0, W1_SPLIT[o])
             deal(scalar_cast(nc), w1_bf[o], w1_raw[o], W1_SPLIT[o], P)
             nc.vector.quantize_mx(out=w1_code[o][:].bitcast(FP8X4), scales=w1_scale[o][:], in_=w1_bf[o][:])
+
+        quantise_w1(0)
         nc.vector.tensor_copy(out=x_code[0][:], in_=word_table[0][:].indirect(offs_sb[:]))
         for t in range(PACK):
             first_product(0, t)
+        quantise_w1(1)
         for a, b in X_CUTS:
             nc.vector.tensor_copy(out=x_code[1][:, a:b], in_=word_table[1][:].indirect(offs_sb[:, a // 16 : b // 16]))
         for t in range(PACK):
@@ -146,8 +149,10 @@ def tile_picked_yserial_none_po_kernel(
         gain = keep.tile([P, PACK], F32, name="gain")
         nc.scalar.activation(out=gain[:], in_=taps_sb[:, :, 0], func=COPY, bias=1.0)
 
-        far = [keep.tile([P, S], F32, name="far%d" % t, align_bytes=64) for t in range(PACK)]
-        near = [keep.tile([P, S], F32, name="near%d" % t, align_bytes=64) for t in range(PACK)]
+        far_tags = ("far0", "far0", "w2_bf", "near1")
+        far = [keep.tile([P, S], F32, name="far%d" % t, tag=far_tags[t], align_bytes=64) for t in range(PACK)]
+        near = [keep.tile([P, S], F32, name="near%d" % t, tag="near%d" % t, align_bytes=64) for t in range(PACK - 1)]
+        own = keep.tile([P, S], F32, name="own", align_bytes=64)
         rr = [keep.tile([P, S], F32, name="rr%d" % t, align_bytes=64) for t in range(PACK)]
         w2_code = keep.tile([P, N], U32, name="w2_code", align_bytes=64)
         w2_scale = keep.tile([P, N], U8, name="w2_scale", align_bytes=64)
@@ -172,7 +177,7 @@ def tile_picked_yserial_none_po_kernel(
 
         def near_tap(t):
             nc.vector.scalar_tensor_tensor(
-                out=near[t][:], in0=gg[t][:, LEAD - 1 : LEAD - 1 + S], scalar=taps_sb[:, t, 1:2], in1=far[t][:],
+                out=(near + rr[3:])[t][:], in0=gg[t][:, LEAD - 1 : LEAD - 1 + S], scalar=taps_sb[:, t, 1:2], in1=far[t][:],
                 op0=MULT, op1=ADD,
             )
 
@@ -185,7 +190,7 @@ def tile_picked_yserial_none_po_kernel(
         def deal_w2(n):
             deal(nc.vector.tensor_copy, w2_bf, w2_raw, 32 * n, 32 * n + 32)
 
-        z = [keep.tile([P, PACK, b - a], BF16, name="z%d" % a, align_bytes=64) for a, b in HALVES]
+        z = [keep.tile([P, PACK, b - a], F32, name="z%d" % a, tag="near2" if a else "z0", align_bytes=64) for a, b in HALVES]
         z_bf = keep.tile([P, PACK * S], BF16, name="z_bf", align_bytes=64)
         z_code = [keep.tile([P, b - a], U32, name="z_code%d" % a, align_bytes=64) for a, b in PIECES]
         z_scale = [keep.tile([P, b - a], U8, name="z_scale%d" % a, align_bytes=64) for a, b in PIECES]
@@ -195,7 +200,11 @@ def tile_picked_yserial_none_po_kernel(
         res_scale = keep.tile([P, S], U8, name="res_scale", align_bytes=64)
         out_rows = out_0.rearrange("(p t) j -> p t j", t=PACK)
         out_words = out_1[0].rearrange("p c r -> p (c r)").bitcast(I32)
-        bank = [psum.tile([P, PACK, b - a], F32, name="res_ps%d" % i, tag="res_ps%d" % i if i < 2 else "y_ps%d" % (i - 2)) for i, (a, b) in enumerate(PIECES)]
+        bank_tags = (("res_ps0",), ("res_ps1",), ("y_ps0",), ("y_ps1", "y_ps2"))
+        bank = [
+            [psum.tile([P, PACK // len(tags), P], F32, name="res_ps%d_%d" % (i, n), tag=tag) for n, tag in enumerate(tags)]
+            for i, tags in enumerate(bank_tags)
+        ]
 
         def z_part(a, b):
             h = a // 256
@@ -203,6 +212,11 @@ def tile_picked_yserial_none_po_kernel(
 
         def by_back(gather, t, a, b):
             gather(z_part(a, b)[:, t, :], rr[t][:], back_sb[:, a // 16 : b // 16])
+
+        def by_back_with_own(a, b):
+            nc.vector.tensor_tensor(
+                out=z_part(a, b)[:, 3, :], in0=rr[3][:].indirect(back_sb[:, a // 16 : b // 16]), in1=own[:, a:b], op=ADD
+            )
 
         def weave_z(i, engine_copy):
             a, b = PIECES[i]
@@ -214,7 +228,7 @@ def tile_picked_yserial_none_po_kernel(
             for t in range(PACK):
                 cols = slice(t * P, (t + 1) * P)
                 nc.tensor.matmul_mx(
-                    out=bank[i][:, t, :],
+                    out=bank[i][t * len(bank[i]) // PACK][:, t % (PACK // len(bank[i])), :],
                     lhsT=w2_code[:, cols].bitcast(FP8X4),
                     lhsT_scale=w2_scale[:, cols],
                     rhs=z_code[i][:].bitcast(FP8X4),
@@ -223,41 +237,45 @@ def tile_picked_yserial_none_po_kernel(
                     stop=True,
                 )
 
-        def round_bank(i, engine_copy):
-            a, b = PIECES[i]
-            weave(engine_copy, res_bf[:, PACK * a : PACK * b], bank[i][:])
-
         def round_stored(i, engine_copy):
             a, b = PIECES[i]
             weave_by_lines(engine_copy, res_bf[:, PACK * a : PACK * b], res[i][:])
 
         def store_res(i):
             a, b = PIECES[i]
-            nc.scalar.copy(out=res[i][:], in_=bank[i][:])
+            planes = PACK // len(bank[i])
+            for n, part in enumerate(bank[i]):
+                nc.scalar.copy(out=res[i][:, n * planes : (n + 1) * planes, :], in_=part[:])
             nc.sync.dma_start(out=out_rows[:, :, a:b], in_=res[i][:])
 
-        def hand_on(h):
-            a, b = HALVES[h]
+        def hand_on(a, b):
             nc.vector.quantize_mx(
                 out=res_code[:, a:b].bitcast(FP8X4), scales=res_scale[:, a:b], in_=res_bf[:, PACK * a : PACK * b]
             )
 
+        def store_codes(a, b):
+            nc.sync.dma_start(out=out_words[:, a:b], in_=res_code[:, a:b].bitcast(I32))
+
         leave_psum(0, nc.scalar.copy)
         leave_psum(1, nc.scalar.copy)
         leave_psum(2, nc.vector.tensor_copy)
+        leave_psum(3, nc.scalar.copy)
         by_order(vector_gather, 0, 0, 256)
         by_order(scalar_gather, 0, 256, 512)
         for t in range(1, PACK):
-            leave_psum(t + 2, nc.scalar.copy)
+            if t < PACK - 1:
+                leave_psum(t + 3, nc.scalar.copy)
             by_order(scalar_gather, t, 0, S)
+        nc.scalar.activation(out=own[:], in_=y_ps[5][:], func=COPY, scale=gain[:, 3:4])
         deal_w2(0)
-        far_tap(0)
         deal_w2(1)
-        near_tap(0)
+        far_tap(0)
         deal_w2(2)
+        near_tap(0)
+        deal_w2(3)
         own_tap(0)
         far_tap(1)
-        deal_w2(3)
+        nc.vector.quantize_mx(out=w2_code[:].bitcast(FP8X4), scales=w2_scale[:], in_=w2_bf[:])
         near_tap(1)
         far_tap(2)
         own_tap(1)
@@ -265,20 +283,16 @@ def tile_picked_yserial_none_po_kernel(
         far_tap(3)
         own_tap(2)
         near_tap(3)
-        nc.vector.quantize_mx(out=w2_code[:].bitcast(FP8X4), scales=w2_scale[:], in_=w2_bf[:])
-        own_tap(3)
-        for t in range(3):
-            by_back(scalar_gather, t, 0, 256)
-        for t in range(2):
-            by_back(scalar_gather, t, 256, 512)
-        by_back(vector_gather, 3, 0, 128)
-        by_back(scalar_gather, 3, 128, 256)
-        by_back(scalar_gather, 2, 256, 512)
-        by_back(scalar_gather, 3, 256, 384)
-        by_back(scalar_gather, 3, 384, 512)
+        for a, b in HALVES:
+            for t in range(3):
+                by_back(scalar_gather, t, a, b)
+        by_back_with_own(0, 128)
+        by_back_with_own(128, 256)
         weave_z(0, nc.vector.tensor_copy)
-        weave_z(1, nc.vector.tensor_copy)
+        by_back_with_own(256, 384)
         second_product(0)
+        weave_z(1, nc.vector.tensor_copy)
+        by_back_with_own(384, 512)
         second_product(1)
         weave_z(2, nc.vector.tensor_copy)
         weave_z(3, nc.vector.tensor_copy)
@@ -289,12 +303,14 @@ def tile_picked_yserial_none_po_kernel(
         store_res(1)
         round_stored(1, nc.vector.tensor_copy)
         store_res(2)
-        hand_on(0)
+        hand_on(0, 256)
+        store_codes(0, 256)
         round_stored(2, nc.vector.tensor_copy)
-        round_bank(3, nc.vector.tensor_copy)
         store_res(3)
-        hand_on(1)
-        nc.sync.dma_start(out=out_words, in_=res_code[:].bitcast(I32))
+        hand_on(256, 384)
+        round_stored(3, nc.vector.tensor_copy)
+        hand_on(384, 512)
+        store_codes(256, 512)
         for q in range(4):
             queue = nc.sync if q % 2 else nc.scalar
             queue.dma_start(

@@ -23,7 +23,7 @@ PASSES = K // K_PASS
 Y_WINDOW = 528
 LEAD = 4
 PIECES = ((0, 128), (128, 256), (256, 384), (384, 512))
-HALVES = ((0, 256), (256, 512))
+HALVES = ((0, 384), (384, 512))
 X_CUTS = ((0, 256), (256, 384), (384, 512))
 W1_SPLIT = (32, 80)
 
@@ -69,7 +69,7 @@ def tile_picked_yserial_none_po_kernel(
         scale_table = keep.tile([P, T], U8, name="scale_table", tag="table1", align_bytes=64)
         word_table = [keep.tile([P, T], U32, name="word_table%d" % o, tag="table%d" % o, align_bytes=64) for o in range(PASSES)]
         w1_raw = [keep.tile([P, PACK, H], F32, name="w1_raw%d" % o, tag="raw%d" % o, align_bytes=64) for o in range(PASSES)]
-        w2_raw = keep.tile([P, PACK, N], F32, name="w2_raw", tag="raw0", align_bytes=64)
+        w2_raw = [keep.tile([P, PACK, N // 2], F32, name="w2_raw%d" % h, tag="raw%d" % h, align_bytes=64) for h in range(2)]
         taps_sb = keep.tile([P, PACK, 3], F32, name="taps_sb")
         picked = keep.tile([P, S], U8, name="picked", align_bytes=64)
         x_scale = keep.tile([P, PASSES, S], U8, name="x_scale", align_bytes=64)
@@ -99,7 +99,9 @@ def tile_picked_yserial_none_po_kernel(
                 in_=picked[32 * q : 32 * q + 32 : 4, :].bitcast(I32),
             )
         load_words(1)
-        nc.sync.dma_start(out=w2_raw[:], in_=w2.rearrange("(p j) c -> p j c", j=PACK))
+        w2_rows = w2.rearrange("(p j) c -> p j c", j=PACK)
+        for h in range(2):
+            nc.sync.dma_start(out=w2_raw[h][:], in_=w2_rows[:, :, h * N // 2 : (h + 1) * N // 2])
         nc.sync.dma_start(out=back_sb[:], in_=back)
 
         y = [keep.tile([P, Y_WINDOW if t else S], F32, name="y%d" % t, align_bytes=64) for t in range(PACK)]
@@ -149,12 +151,12 @@ def tile_picked_yserial_none_po_kernel(
         gain = keep.tile([P, PACK], F32, name="gain")
         nc.scalar.activation(out=gain[:], in_=taps_sb[:, :, 0], func=COPY, bias=1.0)
 
-        far_tags = ("far0", "far0", "w2_bf", "near1")
+        far_tags = ("far0", "raw1", "near0", "near1")
         far = [keep.tile([P, S], F32, name="far%d" % t, tag=far_tags[t], align_bytes=64) for t in range(PACK)]
         near = [keep.tile([P, S], F32, name="near%d" % t, tag="near%d" % t, align_bytes=64) for t in range(PACK - 1)]
         own = keep.tile([P, S], F32, name="own", align_bytes=64)
         rr = [keep.tile([P, S], F32, name="rr%d" % t, align_bytes=64) for t in range(PACK)]
-        w2_code = keep.tile([P, N], U32, name="w2_code", align_bytes=64)
+        w2_code = keep.tile([P, N], U32, name="w2_code", tag="near2", align_bytes=64)
         w2_scale = keep.tile([P, N], U8, name="w2_scale", align_bytes=64)
 
         def vector_gather(out, window, offsets):
@@ -188,9 +190,9 @@ def tile_picked_yserial_none_po_kernel(
             )
 
         def deal_w2(n):
-            deal(nc.vector.tensor_copy, w2_bf, w2_raw, 32 * n, 32 * n + 32)
+            deal(nc.vector.tensor_copy, w2_bf, w2_raw[n // 2], 32 * n, 32 * n + 32, base=64 * (n // 2))
 
-        z = [keep.tile([P, PACK, b - a], F32, name="z%d" % a, tag="near2" if a else "z0", align_bytes=64) for a, b in HALVES]
+        z = [keep.tile([P, PACK, b - a], F32, name="z%d" % a, tag="near1" if a else "z0", align_bytes=64) for a, b in HALVES]
         z_bf = keep.tile([P, PACK * S], BF16, name="z_bf", align_bytes=64)
         z_code = [keep.tile([P, b - a], U32, name="z_code%d" % a, align_bytes=64) for a, b in PIECES]
         z_scale = [keep.tile([P, b - a], U8, name="z_scale%d" % a, align_bytes=64) for a, b in PIECES]
@@ -207,8 +209,8 @@ def tile_picked_yserial_none_po_kernel(
         ]
 
         def z_part(a, b):
-            h = a // 256
-            return z[h][:, :, a - 256 * h : b - 256 * h]
+            h = a // HALVES[1][0]
+            return z[h][:, :, a - HALVES[h][0] : b - HALVES[h][0]]
 
         def by_back(gather, t, a, b):
             gather(z_part(a, b)[:, t, :], rr[t][:], back_sb[:, a // 16 : b // 16])
@@ -258,24 +260,23 @@ def tile_picked_yserial_none_po_kernel(
 
         leave_psum(0, nc.scalar.copy)
         leave_psum(1, nc.scalar.copy)
+        deal_w2(0)
         leave_psum(2, nc.vector.tensor_copy)
+        deal_w2(1)
         leave_psum(3, nc.scalar.copy)
         by_order(vector_gather, 0, 0, 256)
-        by_order(scalar_gather, 0, 256, 512)
+        by_order(vector_gather, 0, 256, 512)
         for t in range(1, PACK):
             if t < PACK - 1:
                 leave_psum(t + 3, nc.scalar.copy)
             by_order(scalar_gather, t, 0, S)
         nc.scalar.activation(out=own[:], in_=y_ps[5][:], func=COPY, scale=gain[:, 3:4])
-        deal_w2(0)
-        deal_w2(1)
-        far_tap(0)
         deal_w2(2)
-        near_tap(0)
+        far_tap(0)
         deal_w2(3)
-        own_tap(0)
+        near_tap(0)
         far_tap(1)
-        nc.vector.quantize_mx(out=w2_code[:].bitcast(FP8X4), scales=w2_scale[:], in_=w2_bf[:])
+        own_tap(0)
         near_tap(1)
         far_tap(2)
         own_tap(1)
@@ -283,6 +284,7 @@ def tile_picked_yserial_none_po_kernel(
         far_tap(3)
         own_tap(2)
         near_tap(3)
+        nc.vector.quantize_mx(out=w2_code[:].bitcast(FP8X4), scales=w2_scale[:], in_=w2_bf[:])
         for a, b in HALVES:
             for t in range(3):
                 by_back(scalar_gather, t, a, b)

@@ -119,19 +119,18 @@ def tile_picked_yserial_none_po_kernel(
         y_ps = [psum.tile([P, b - a], F32, name="y_ps%d" % n, tag="y_ps%d" % n) for n, (t, a, b) in enumerate(y_parts)]
         w2_bf = keep.tile([P, PACK * N], BF16, name="w2_bf", tag="w2_bf", align_bytes=64)
 
-        def first_product(o, t):
+        def product_pass(o, n, a, b, stop):
+            t, base, end = y_parts[n]
             cols = slice(t * P, (t + 1) * P)
-            for n, (owner, a, b) in enumerate(y_parts):
-                if owner == t:
-                    nc.tensor.matmul_mx(
-                        out=y_ps[n][:],
-                        lhsT=w1_code[o][:, cols].bitcast(FP8X4),
-                        lhsT_scale=w1_scale[o][:, cols],
-                        rhs=x_code[o][:, a:b].bitcast(FP8X4),
-                        rhs_scale=x_scale[:, o, a:b],
-                        start=(o == 0),
-                        stop=(o == PASSES - 1),
-                    )
+            nc.tensor.matmul_mx(
+                out=y_ps[n][:, a - base : b - base],
+                lhsT=w1_code[o][:, cols].bitcast(FP8X4),
+                lhsT_scale=w1_scale[o][:, cols],
+                rhs=x_code[o][:, a:b].bitcast(FP8X4),
+                rhs_scale=x_scale[:, o, a:b],
+                start=(o == 0),
+                stop=stop,
+            )
 
         def quantise_w1(o):
             deal(nc.vector.tensor_copy, w1_bf[o], w1_raw[o], 0, W1_SPLIT[o])
@@ -140,13 +139,18 @@ def tile_picked_yserial_none_po_kernel(
 
         quantise_w1(0)
         nc.vector.tensor_copy(out=x_code[0][:], in_=word_table[0][:].indirect(offs_sb[:]))
-        for t in range(PACK):
-            first_product(0, t)
+        for n, (t, a, b) in enumerate(y_parts):
+            product_pass(0, n, a, b, False)
         quantise_w1(1)
         for a, b in X_CUTS:
             nc.vector.tensor_copy(out=x_code[1][:, a:b], in_=word_table[1][:].indirect(offs_sb[:, a // 16 : b // 16]))
-        for t in range(PACK):
-            first_product(1, t)
+        product_pass(1, 0, 0, 256, True)
+        product_pass(1, 3, 0, 256, False)
+        product_pass(1, 1, 256, 384, True)
+        product_pass(1, 2, 384, 512, True)
+        product_pass(1, 3, 256, 512, True)
+        product_pass(1, 4, 0, 512, True)
+        product_pass(1, 5, 0, 512, True)
 
         gain = keep.tile([P, PACK], F32, name="gain")
         nc.scalar.activation(out=gain[:], in_=taps_sb[:, :, 0], func=COPY, bias=1.0)
@@ -189,8 +193,8 @@ def tile_picked_yserial_none_po_kernel(
                 op0=MULT, op1=ADD,
             )
 
-        def deal_w2(n):
-            deal(nc.vector.tensor_copy, w2_bf, w2_raw[n // 2], 32 * n, 32 * n + 32, base=64 * (n // 2))
+        def deal_w2(m0, m1):
+            deal(nc.vector.tensor_copy, w2_bf, w2_raw[m0 // 64], m0, m1, base=64 * (m0 // 64))
 
         z = [keep.tile([P, PACK, b - a], F32, name="z%d" % a, tag="near1" if a else "z0", align_bytes=64) for a, b in HALVES]
         z_bf = keep.tile([P, PACK * S], BF16, name="z_bf", align_bytes=64)
@@ -260,9 +264,8 @@ def tile_picked_yserial_none_po_kernel(
 
         leave_psum(0, nc.scalar.copy)
         leave_psum(1, nc.scalar.copy)
-        deal_w2(0)
-        leave_psum(2, nc.vector.tensor_copy)
-        deal_w2(1)
+        leave_psum(2, nc.scalar.copy)
+        deal_w2(0, 64)
         leave_psum(3, nc.scalar.copy)
         by_order(vector_gather, 0, 0, 256)
         by_order(vector_gather, 0, 256, 512)
@@ -271,9 +274,9 @@ def tile_picked_yserial_none_po_kernel(
                 leave_psum(t + 3, nc.scalar.copy)
             by_order(scalar_gather, t, 0, S)
         nc.scalar.activation(out=own[:], in_=y_ps[5][:], func=COPY, scale=gain[:, 3:4])
-        deal_w2(2)
+        deal_w2(64, 104)
         far_tap(0)
-        deal_w2(3)
+        deal_w2(104, 128)
         near_tap(0)
         far_tap(1)
         own_tap(0)

@@ -25,7 +25,7 @@ LEAD = 4
 PIECES = ((0, 128), (128, 256), (256, 384), (384, 512))
 HALVES = ((0, 384), (384, 512))
 X_CUTS = ((0, 256), (256, 384), (384, 512))
-W1_SPLIT = (32, 80)
+W1_SPLIT = (32, 64)
 
 
 def deal(engine_copy, grouped, raw, m0, m1, base=0):
@@ -88,8 +88,8 @@ def tile_picked_yserial_none_po_kernel(
         for o in range(PASSES):
             nc.sync.dma_start(out=scale_table[4 * o : P : 8, :].bitcast(I32), in_=x_scales[o].bitcast(I32))
         nc.sync.dma_start(out=offs_sb[:], in_=offs)
-        load_words(0)
         nc.sync.dma_start(out=w1_raw[1][:], in_=w1_rows[1])
+        load_words(0)
         nc.sync.dma_start(out=taps_sb[:], in_=taps.rearrange("(p t) e -> p t e", t=PACK))
         nc.sync.dma_start(out=order_sb[:], in_=order)
         nc.vector.tensor_copy(out=picked[:], in_=scale_table[:].indirect(offs_sb[:]))
@@ -119,7 +119,7 @@ def tile_picked_yserial_none_po_kernel(
         y_ps = [psum.tile([P, b - a], F32, name="y_ps%d" % n, tag="y_ps%d" % n) for n, (t, a, b) in enumerate(y_parts)]
         w2_bf = keep.tile([P, PACK * N], BF16, name="w2_bf", tag="w2_bf", align_bytes=64)
 
-        def product_pass(o, n, a, b, stop):
+        def product_pass(o, n, a, b, start, stop):
             t, base, end = y_parts[n]
             cols = slice(t * P, (t + 1) * P)
             nc.tensor.matmul_mx(
@@ -128,7 +128,7 @@ def tile_picked_yserial_none_po_kernel(
                 lhsT_scale=w1_scale[o][:, cols],
                 rhs=x_code[o][:, a:b].bitcast(FP8X4),
                 rhs_scale=x_scale[:, o, a:b],
-                start=(o == 0),
+                start=start,
                 stop=stop,
             )
 
@@ -138,19 +138,21 @@ def tile_picked_yserial_none_po_kernel(
             nc.vector.quantize_mx(out=w1_code[o][:].bitcast(FP8X4), scales=w1_scale[o][:], in_=w1_bf[o][:])
 
         quantise_w1(0)
-        nc.vector.tensor_copy(out=x_code[0][:], in_=word_table[0][:].indirect(offs_sb[:]))
-        for n, (t, a, b) in enumerate(y_parts):
-            product_pass(0, n, a, b, False)
         quantise_w1(1)
+        for a, b in ((0, 256), (256, 512)):
+            nc.vector.tensor_copy(out=x_code[0][:, a:b], in_=word_table[0][:].indirect(offs_sb[:, a // 16 : b // 16]))
+            for n, (t, base, end) in enumerate(y_parts):
+                if base < b and end > a:
+                    product_pass(0, n, max(a, base), min(b, end), base >= a, False)
         for a, b in X_CUTS:
             nc.vector.tensor_copy(out=x_code[1][:, a:b], in_=word_table[1][:].indirect(offs_sb[:, a // 16 : b // 16]))
-        product_pass(1, 0, 0, 256, True)
-        product_pass(1, 3, 0, 256, False)
-        product_pass(1, 1, 256, 384, True)
-        product_pass(1, 2, 384, 512, True)
-        product_pass(1, 3, 256, 512, True)
-        product_pass(1, 4, 0, 512, True)
-        product_pass(1, 5, 0, 512, True)
+        product_pass(1, 0, 0, 256, False, True)
+        product_pass(1, 3, 0, 256, False, False)
+        product_pass(1, 1, 256, 384, False, True)
+        product_pass(1, 2, 384, 512, False, True)
+        product_pass(1, 3, 256, 512, False, True)
+        product_pass(1, 4, 0, 512, False, True)
+        product_pass(1, 5, 0, 512, False, True)
 
         gain = keep.tile([P, PACK], F32, name="gain")
         nc.scalar.activation(out=gain[:], in_=taps_sb[:, :, 0], func=COPY, bias=1.0)

@@ -301,7 +301,7 @@ def tile_picked_yserial_none_po_kernel(
         weave_z(1, nc.vector.tensor_copy)
         by_back_with_own(384, 512)
         second_product(1)
-        weave_z(2, nc.vector.tensor_copy)
+        weave_z(2, nc.scalar.copy)
         weave_z(3, nc.vector.tensor_copy)
         second_product(2)
         second_product(3)
@@ -311,13 +311,12 @@ def tile_picked_yserial_none_po_kernel(
         round_stored(1, nc.vector.tensor_copy)
         store_res(2)
         hand_on(0, 256)
-        store_codes(0, 256)
         round_stored(2, nc.vector.tensor_copy)
         store_res(3)
-        hand_on(256, 384)
         round_stored(3, nc.vector.tensor_copy)
+        hand_on(256, 384)
         hand_on(384, 512)
-        store_codes(256, 512)
+        store_codes(0, 512)
         for q in range(4):
             queue = nc.sync if q % 2 else nc.scalar
             queue.dma_start(

@@ -208,7 +208,7 @@ def tile_picked_yserial_none_po_kernel(
         res_scale = keep.tile([P, S], U8, name="res_scale", align_bytes=64)
         out_rows = out_0.rearrange("(p t) j -> p t j", t=PACK)
         out_words = out_1[0].rearrange("p c r -> p (c r)").bitcast(I32)
-        bank_tags = (("res_ps0",), ("res_ps1",), ("y_ps0",), ("y_ps1", "y_ps2"))
+        bank_tags = (("res_ps0", "res_ps1"), ("y_ps0", "y_ps1"), ("y_ps2", "y_ps3"), ("y_ps4", "y_ps5"))
         bank = [
             [psum.tile([P, PACK // len(tags), P], F32, name="res_ps%d_%d" % (i, n), tag=tag) for n, tag in enumerate(tags)]
             for i, tags in enumerate(bank_tags)
@@ -245,9 +245,9 @@ def tile_picked_yserial_none_po_kernel(
                     stop=True,
                 )
 
-        def round_stored(i, engine_copy):
-            a, b = PIECES[i]
-            weave_by_lines(engine_copy, res_bf[:, PACK * a : PACK * b], res[i][:])
+        def round_stored(i, engine_copy, c0=0, c1=P):
+            a = PIECES[i][0]
+            weave_by_lines(engine_copy, res_bf[:, PACK * (a + c0) : PACK * (a + c1)], res[i][:, :, c0:c1])
 
         def store_res(i):
             a, b = PIECES[i]
@@ -311,8 +311,9 @@ def tile_picked_yserial_none_po_kernel(
         round_stored(1, nc.vector.tensor_copy)
         store_res(2)
         hand_on(0, 256)
-        round_stored(2, nc.vector.tensor_copy)
+        round_stored(2, nc.vector.tensor_copy, 0, 64)
         store_res(3)
+        round_stored(2, nc.scalar.copy, 64, P)
         round_stored(3, nc.vector.tensor_copy)
         hand_on(256, 384)
         hand_on(384, 512)

@@ -18,14 +18,20 @@ ADD = mybir.AluOpType.add
 
 P = 128
 PACK = 4
-K_PASS = P * PACK
-PASSES = K // K_PASS
-Y_WINDOW = 528
+PASSES = K // (P * PACK)
+LAST = PACK - 1
+PER_COLUMN = 16
+
+Y_WINDOW = (704, 528, 528, 528)
 LEAD = 4
-PIECES = ((0, 128), (128, 256), (256, 384), (384, 512))
-HALVES = ((0, 384), (384, 512))
+HALVES = ((0, S // 2), (S // 2, S))
 X_CUTS = ((0, 256), (256, 384), (384, 512))
-W1_SPLIT = (32, 64)
+PIECES = ((0, 128), (128, 256), (256, 384), (384, 512))
+Z_PARTS = ((0, 384), (384, 512))
+W1_ON_VECTOR = (32, 64)
+W2_PARTS = ((0, 64), (64, 96), (96, 128))
+W2_CUT = 112
+PIECE_2_ON_VECTOR = 64
 
 
 def deal(engine_copy, grouped, raw, m0, m1, base=0):
@@ -35,22 +41,15 @@ def deal(engine_copy, grouped, raw, m0, m1, base=0):
     )
 
 
-def scalar_cast(nc):
-    return lambda out, in_: nc.scalar.activation(out=out, in_=in_, func=COPY)
-
-
 def weave(engine_copy, woven, planes):
-    engine_copy(
-        out=woven.rearrange("p (c t) -> p c t", t=PACK),
-        in_=planes.rearrange("p t c -> p c t"),
-    )
-
-
-def weave_by_lines(engine_copy, woven, planes):
     engine_copy(
         out=woven.rearrange("p (c i t) -> p c t i", i=4, t=PACK),
         in_=planes.rearrange("p t (c i) -> p c t i", i=4),
     )
+
+
+def entries(list_tile, a, b):
+    return list_tile[:, a // PER_COLUMN : b // PER_COLUMN]
 
 
 def tile_picked_yserial_none_po_kernel(
@@ -62,17 +61,33 @@ def tile_picked_yserial_none_po_kernel(
         keep = ctx.enter_context(tc.tile_pool(name="keep", bufs=1))
         psum = ctx.enter_context(tc.psum_pool(name="psum", bufs=1))
 
-        offs_sb = lists.tile([P, S // 16], U16, name="offs_sb")
-        order_sb = lists.tile([P, S // 16], U16, name="order_sb")
-        back_sb = lists.tile([P, S // 16], U16, name="back_sb")
+        def tile(shape, dtype, name, tag=None):
+            return keep.tile(shape, dtype, name=name, tag=tag or name, align_bytes=64)
 
-        scale_table = keep.tile([P, T], U8, name="scale_table", tag="table1", align_bytes=64)
-        word_table = [keep.tile([P, T], U32, name="word_table%d" % o, tag="table%d" % o, align_bytes=64) for o in range(PASSES)]
-        w1_raw = [keep.tile([P, PACK, H], F32, name="w1_raw%d" % o, tag="raw%d" % o, align_bytes=64) for o in range(PASSES)]
-        w2_raw = [keep.tile([P, PACK, N // 2], F32, name="w2_raw%d" % h, tag="raw%d" % h, align_bytes=64) for h in range(2)]
+        def scalar_cast(out, in_):
+            nc.scalar.activation(out=out, in_=in_, func=COPY)
+
+        def vector_gather(out, window, offsets):
+            nc.vector.tensor_copy(out=out, in_=window.indirect(offsets))
+
+        def scalar_gather(out, window, offsets):
+            nc.scalar.activation(out=out, in_=window.indirect(offsets), func=COPY)
+
+        def quantise(code, scale, woven):
+            nc.vector.quantize_mx(out=code.bitcast(FP8X4), scales=scale, in_=woven)
+
+        offs_sb = lists.tile([P, S // PER_COLUMN], U16, name="offs_sb")
+        order_sb = lists.tile([P, S // PER_COLUMN], U16, name="order_sb")
+        back_sb = lists.tile([P, S // PER_COLUMN], U16, name="back_sb")
+
+        scale_table = tile([P, T], U8, "scale_table", tag="table1")
+        word_table = [tile([P, T], U32, "word_table%d" % o, tag="table%d" % o) for o in range(PASSES)]
+        w1_raw = [tile([P, PACK, H], F32, "w1_raw%d" % o, tag="raw%d" % o) for o in range(PASSES)]
+        w2_tags = ("raw0", "raw1", "table0")
+        w2_raw = [tile([P, PACK, PACK * (m1 - m0)], F32, "w2_raw%d" % m0, tag=w2_tags[h]) for h, (m0, m1) in enumerate(W2_PARTS)]
         taps_sb = keep.tile([P, PACK, 3], F32, name="taps_sb")
-        picked = keep.tile([P, S], U8, name="picked", align_bytes=64)
-        x_scale = keep.tile([P, PASSES, S], U8, name="x_scale", align_bytes=64)
+        picked_scale = tile([P, S], U8, "picked_scale")
+        x_scale = tile([P, PASSES, S], U8, "x_scale")
 
         nc.vector.memset(scale_table[:, 0 : T // 2].bitcast(I32), 0)
         nc.gpsimd.memset(scale_table[:, T // 2 : T].bitcast(I32), 0)
@@ -92,151 +107,161 @@ def tile_picked_yserial_none_po_kernel(
         load_words(0)
         nc.sync.dma_start(out=taps_sb[:], in_=taps.rearrange("(p t) e -> p t e", t=PACK))
         nc.sync.dma_start(out=order_sb[:], in_=order)
-        nc.vector.tensor_copy(out=picked[:], in_=scale_table[:].indirect(offs_sb[:]))
+        vector_gather(picked_scale[:], scale_table[:], offs_sb[:])
         for q in range(4):
             nc.sync.dma_start(
                 out=x_scale[32 * q : 32 * q + 4].rearrange("r o c -> r (o c)").bitcast(I32),
-                in_=picked[32 * q : 32 * q + 32 : 4, :].bitcast(I32),
+                in_=picked_scale[32 * q : 32 * q + 32 : 4, :].bitcast(I32),
             )
         load_words(1)
         w2_rows = w2.rearrange("(p j) c -> p j c", j=PACK)
-        for h in range(2):
-            nc.sync.dma_start(out=w2_raw[h][:], in_=w2_rows[:, :, h * N // 2 : (h + 1) * N // 2])
+        for h, (m0, m1) in enumerate(W2_PARTS):
+            nc.sync.dma_start(out=w2_raw[h][:], in_=w2_rows[:, :, PACK * m0 : PACK * m1])
         nc.sync.dma_start(out=back_sb[:], in_=back)
 
-        y = [keep.tile([P, Y_WINDOW if t else S], F32, name="y%d" % t, align_bytes=64) for t in range(PACK)]
-        gg = [keep.tile([P, LEAD + S], F32, name="gg%d" % t, align_bytes=64) for t in range(PACK)]
+        y = [tile([P, Y_WINDOW[t]], F32, "y%d" % t) for t in range(PACK)]
+        gg = [tile([P, LEAD + S], F32, "gg%d" % t) for t in range(PACK)]
         for t in range(PACK):
-            if t:
-                nc.vector.memset(y[t][:, S:Y_WINDOW], 0.0)
-            nc.vector.memset(gg[t][:, 0:LEAD], 0.0)
+            nc.vector.memset(y[t][:, S : Y_WINDOW[t]], 0.0)
+            nc.vector.memset(gg[t][:, LEAD - 2 : LEAD], 0.0)
 
-        x_code = [keep.tile([P, S], U32, name="x_code%d" % o, align_bytes=64) for o in range(PASSES)]
-        w1_code = [keep.tile([P, H], U32, name="w1_code%d" % o, align_bytes=64) for o in range(PASSES)]
-        w1_scale = [keep.tile([P, H], U8, name="w1_scale%d" % o, align_bytes=64) for o in range(PASSES)]
-        w1_bf = [keep.tile([P, PACK * H], BF16, name="w1_bf%d" % o, tag="w1_bf%d" % o, align_bytes=64) for o in range(PASSES)]
-        y_parts = [(0, a, b) for a, b in X_CUTS] + [(t, 0, S) for t in range(1, PACK)]
-        y_ps = [psum.tile([P, b - a], F32, name="y_ps%d" % n, tag="y_ps%d" % n) for n, (t, a, b) in enumerate(y_parts)]
-        w2_bf = keep.tile([P, PACK * N], BF16, name="w2_bf", tag="w2_bf", align_bytes=64)
+        x_code = [tile([P, S], U32, "x_code%d" % o) for o in range(PASSES)]
+        w1_code = [tile([P, H], U32, "w1_code%d" % o) for o in range(PASSES)]
+        w1_scale = [tile([P, H], U8, "w1_scale%d" % o) for o in range(PASSES)]
+        w1_bf = [tile([P, PACK * H], BF16, "w1_bf%d" % o) for o in range(PASSES)]
+        y_banks = [(0, a, b) for a, b in X_CUTS] + [(t, 0, S) for t in range(1, PACK)]
+        y_ps = [psum.tile([P, b - a], F32, name="y_ps%d" % n, tag="y_ps%d" % n) for n, (t, a, b) in enumerate(y_banks)]
+        bank_of_plane = {t: n for n, (t, a, b) in enumerate(y_banks) if t > 0}
+        w2_bf = tile([P, PACK * N], BF16, "w2_bf")
 
-        def product_pass(o, n, a, b, start, stop):
-            t, base, end = y_parts[n]
+        def first_product(o, n, a, b):
+            t, first, end = y_banks[n]
             cols = slice(t * P, (t + 1) * P)
             nc.tensor.matmul_mx(
-                out=y_ps[n][:, a - base : b - base],
+                out=y_ps[n][:, a - first : b - first],
                 lhsT=w1_code[o][:, cols].bitcast(FP8X4),
                 lhsT_scale=w1_scale[o][:, cols],
                 rhs=x_code[o][:, a:b].bitcast(FP8X4),
                 rhs_scale=x_scale[:, o, a:b],
-                start=start,
-                stop=stop,
+                start=(o == 0 and a == first),
+                stop=(o == PASSES - 1 and b == end),
             )
 
-        def quantise_w1(o):
-            deal(nc.vector.tensor_copy, w1_bf[o], w1_raw[o], 0, W1_SPLIT[o])
-            deal(scalar_cast(nc), w1_bf[o], w1_raw[o], W1_SPLIT[o], P)
-            nc.vector.quantize_mx(out=w1_code[o][:].bitcast(FP8X4), scales=w1_scale[o][:], in_=w1_bf[o][:])
-
-        quantise_w1(0)
-        quantise_w1(1)
-        for a, b in ((0, 256), (256, 512)):
-            nc.vector.tensor_copy(out=x_code[0][:, a:b], in_=word_table[0][:].indirect(offs_sb[:, a // 16 : b // 16]))
-            for n, (t, base, end) in enumerate(y_parts):
-                if base < b and end > a:
-                    product_pass(0, n, max(a, base), min(b, end), base >= a, False)
+        for o in range(PASSES):
+            deal(nc.vector.tensor_copy, w1_bf[o], w1_raw[o], 0, W1_ON_VECTOR[o])
+            deal(scalar_cast, w1_bf[o], w1_raw[o], W1_ON_VECTOR[o], P)
+            quantise(w1_code[o][:], w1_scale[o][:], w1_bf[o][:])
+        for a, b in HALVES:
+            vector_gather(x_code[0][:, a:b], word_table[0][:], entries(offs_sb, a, b))
+            for n, (t, first, end) in enumerate(y_banks):
+                if first < b and end > a:
+                    first_product(0, n, max(a, first), min(b, end))
         for a, b in X_CUTS:
-            nc.vector.tensor_copy(out=x_code[1][:, a:b], in_=word_table[1][:].indirect(offs_sb[:, a // 16 : b // 16]))
-        product_pass(1, 0, 0, 256, False, True)
-        product_pass(1, 3, 0, 256, False, False)
-        product_pass(1, 1, 256, 384, False, True)
-        product_pass(1, 2, 384, 512, False, True)
-        product_pass(1, 3, 256, 512, False, True)
-        product_pass(1, 4, 0, 512, False, True)
-        product_pass(1, 5, 0, 512, False, True)
+            vector_gather(x_code[1][:, a:b], word_table[1][:], entries(offs_sb, a, b))
+        for a, b in HALVES:
+            for n, (first, end) in enumerate(X_CUTS):
+                if a <= first and end <= b:
+                    first_product(1, n, first, end)
+            first_product(1, bank_of_plane[1], a, b)
+        for t in range(2, PACK):
+            first_product(1, bank_of_plane[t], 0, S)
 
         gain = keep.tile([P, PACK], F32, name="gain")
         nc.scalar.activation(out=gain[:], in_=taps_sb[:, :, 0], func=COPY, bias=1.0)
 
-        far_tags = ("far0", "raw1", "near0", "near1")
-        far = [keep.tile([P, S], F32, name="far%d" % t, tag=far_tags[t], align_bytes=64) for t in range(PACK)]
-        near = [keep.tile([P, S], F32, name="near%d" % t, tag="near%d" % t, align_bytes=64) for t in range(PACK - 1)]
-        own = keep.tile([P, S], F32, name="own", align_bytes=64)
-        rr = [keep.tile([P, S], F32, name="rr%d" % t, align_bytes=64) for t in range(PACK)]
-        w2_code = keep.tile([P, N], U32, name="w2_code", tag="near2", align_bytes=64)
-        w2_scale = keep.tile([P, N], U8, name="w2_scale", align_bytes=64)
+        far_tags = ("far0", "table0", "near0", "near1")
+        far = [tile([P, S], F32, "far%d" % t, tag=far_tags[t]) for t in range(PACK)]
+        near = [tile([P, S], F32, "near%d" % t) for t in range(LAST)]
+        own_last = tile([P, S], F32, "own_last")
+        rr = [tile([P, S], F32, "rr%d" % t) for t in range(PACK)]
+        w2_code = tile([P, N], U32, "w2_code", tag="near2")
+        w2_scale = tile([P, N], U8, "w2_scale")
 
-        def vector_gather(out, window, offsets):
-            nc.vector.tensor_copy(out=out, in_=window.indirect(offsets))
-
-        def scalar_gather(out, window, offsets):
-            nc.scalar.activation(out=out, in_=window.indirect(offsets), func=COPY)
-
-        def leave_psum(n, engine_copy):
-            t, a, b = y_parts[n]
+        def leave_psum(n, engine_copy=nc.scalar.copy):
+            t, a, b = y_banks[n]
             engine_copy(out=y[t][:, a:b], in_=y_ps[n][:])
 
-        def by_order(gather, t, a, b):
-            gather(gg[t][:, LEAD + a : LEAD + b], y[t][:], order_sb[:, a // 16 : b // 16])
+        def by_order(gather, t):
+            gather(gg[t][:, LEAD : LEAD + S], y[t][:], order_sb[:])
+
+        def shifted(t, steps):
+            return gg[t][:, LEAD - steps : LEAD - steps + S]
 
         def far_tap(t):
-            nc.vector.tensor_scalar(
-                out=far[t][:], in0=gg[t][:, LEAD - 2 : LEAD - 2 + S], scalar1=taps_sb[:, t, 2:3], scalar2=None, op0=MULT
-            )
+            nc.vector.tensor_scalar(out=far[t][:], in0=shifted(t, 2), scalar1=taps_sb[:, t, 2:3], scalar2=None, op0=MULT)
 
         def near_tap(t):
+            total = rr[t] if t == LAST else near[t]
             nc.vector.scalar_tensor_tensor(
-                out=(near + rr[3:])[t][:], in0=gg[t][:, LEAD - 1 : LEAD - 1 + S], scalar=taps_sb[:, t, 1:2], in1=far[t][:],
-                op0=MULT, op1=ADD,
+                out=total[:], in0=shifted(t, 1), scalar=taps_sb[:, t, 1:2], in1=far[t][:], op0=MULT, op1=ADD
             )
 
         def own_tap(t):
             nc.vector.scalar_tensor_tensor(
-                out=rr[t][:], in0=gg[t][:, LEAD : LEAD + S], scalar=gain[:, t : t + 1], in1=near[t][:],
-                op0=MULT, op1=ADD,
+                out=rr[t][:], in0=shifted(t, 0), scalar=gain[:, t : t + 1], in1=near[t][:], op0=MULT, op1=ADD
             )
 
-        def deal_w2(m0, m1):
-            deal(nc.vector.tensor_copy, w2_bf, w2_raw[m0 // 64], m0, m1, base=64 * (m0 // 64))
+        def deal_w2(h, m0, m1):
+            deal(nc.vector.tensor_copy, w2_bf, w2_raw[h], m0, m1, base=W2_PARTS[h][0])
 
-        z = [keep.tile([P, PACK, b - a], F32, name="z%d" % a, tag="near1" if a else "z0", align_bytes=64) for a, b in HALVES]
-        z_bf = keep.tile([P, PACK * S], BF16, name="z_bf", align_bytes=64)
-        z_code = [keep.tile([P, b - a], U32, name="z_code%d" % a, align_bytes=64) for a, b in PIECES]
-        z_scale = [keep.tile([P, b - a], U8, name="z_scale%d" % a, align_bytes=64) for a, b in PIECES]
-        res = [keep.tile([P, PACK, b - a], F32, name="res%d" % a, align_bytes=64) for a, b in PIECES]
-        res_bf = keep.tile([P, PACK * S], BF16, name="res_bf", align_bytes=64)
-        res_code = keep.tile([P, S], U32, name="res_code", align_bytes=64)
-        res_scale = keep.tile([P, S], U8, name="res_scale", align_bytes=64)
+        leave_psum(0)
+        leave_psum(1)
+        deal_w2(0, *W2_PARTS[0])
+        leave_psum(2, nc.vector.tensor_copy)
+        deal_w2(1, *W2_PARTS[1])
+        leave_psum(bank_of_plane[1])
+        by_order(vector_gather, 0)
+        for t in range(1, PACK):
+            if t < LAST:
+                leave_psum(bank_of_plane[t + 1])
+            by_order(scalar_gather, t)
+        nc.scalar.activation(out=own_last[:], in_=y_ps[bank_of_plane[LAST]][:], func=COPY, scale=gain[:, LAST : LAST + 1])
+        deal_w2(2, W2_PARTS[2][0], W2_CUT)
+        far_tap(0)
+        deal_w2(2, W2_CUT, P)
+        near_tap(0)
+        for t in range(1, PACK):
+            far_tap(t)
+            own_tap(t - 1)
+            near_tap(t)
+        quantise(w2_code[:], w2_scale[:], w2_bf[:])
+
+        z = [tile([P, PACK, b - a], F32, "z%d" % a, tag="near1" if a else None) for a, b in Z_PARTS]
+        z_bf = tile([P, PACK * S], BF16, "z_bf")
+        z_code = [tile([P, b - a], U32, "z_code%d" % a) for a, b in PIECES]
+        z_scale = [tile([P, b - a], U8, "z_scale%d" % a) for a, b in PIECES]
+        res = [tile([P, PACK, b - a], F32, "res%d" % a) for a, b in PIECES]
+        res_bf = tile([P, PACK * S], BF16, "res_bf")
+        res_code = tile([P, S], U32, "res_code")
+        res_scale = tile([P, S], U8, "res_scale")
         out_rows = out_0.rearrange("(p t) j -> p t j", t=PACK)
         out_words = out_1[0].rearrange("p c r -> p (c r)").bitcast(I32)
-        bank_tags = (("res_ps0", "res_ps1"), ("y_ps0", "y_ps1"), ("y_ps2", "y_ps3"), ("y_ps4", "y_ps5"))
-        bank = [
-            [psum.tile([P, PACK // len(tags), P], F32, name="res_ps%d_%d" % (i, n), tag=tag) for n, tag in enumerate(tags)]
-            for i, tags in enumerate(bank_tags)
+        res_tags = ["res_ps0", "res_ps1"] + ["y_ps%d" % n for n in range(len(y_banks))]
+        res_ps = [
+            [psum.tile([P, 2, P], F32, name="res_ps%d_%d" % (i, n), tag=res_tags[2 * i + n]) for n in range(2)]
+            for i in range(len(PIECES))
         ]
 
-        def z_part(a, b):
-            h = a // HALVES[1][0]
-            return z[h][:, :, a - HALVES[h][0] : b - HALVES[h][0]]
+        def z_planes(a, b):
+            part = a // Z_PARTS[1][0]
+            return z[part][:, :, a - Z_PARTS[part][0] : b - Z_PARTS[part][0]]
 
-        def by_back(gather, t, a, b):
-            gather(z_part(a, b)[:, t, :], rr[t][:], back_sb[:, a // 16 : b // 16])
-
-        def by_back_with_own(a, b):
+        def by_back_last_plane(a, b):
             nc.vector.tensor_tensor(
-                out=z_part(a, b)[:, 3, :], in0=rr[3][:].indirect(back_sb[:, a // 16 : b // 16]), in1=own[:, a:b], op=ADD
+                out=z_planes(a, b)[:, LAST, :], in0=rr[LAST][:].indirect(entries(back_sb, a, b)), in1=own_last[:, a:b], op=ADD
             )
 
         def weave_z(i, engine_copy):
             a, b = PIECES[i]
-            weave_by_lines(engine_copy, z_bf[:, PACK * a : PACK * b], z_part(a, b))
+            weave(engine_copy, z_bf[:, PACK * a : PACK * b], z_planes(a, b))
 
         def second_product(i):
             a, b = PIECES[i]
-            nc.vector.quantize_mx(out=z_code[i][:].bitcast(FP8X4), scales=z_scale[i][:], in_=z_bf[:, PACK * a : PACK * b])
+            quantise(z_code[i][:], z_scale[i][:], z_bf[:, PACK * a : PACK * b])
             for t in range(PACK):
                 cols = slice(t * P, (t + 1) * P)
                 nc.tensor.matmul_mx(
-                    out=bank[i][t * len(bank[i]) // PACK][:, t % (PACK // len(bank[i])), :],
+                    out=res_ps[i][t // 2][:, t % 2, :],
                     lhsT=w2_code[:, cols].bitcast(FP8X4),
                     lhsT_scale=w2_scale[:, cols],
                     rhs=z_code[i][:].bitcast(FP8X4),
@@ -245,79 +270,46 @@ def tile_picked_yserial_none_po_kernel(
                     stop=True,
                 )
 
-        def round_stored(i, engine_copy, c0=0, c1=P):
-            a = PIECES[i][0]
-            weave_by_lines(engine_copy, res_bf[:, PACK * (a + c0) : PACK * (a + c1)], res[i][:, :, c0:c1])
-
         def store_res(i):
             a, b = PIECES[i]
-            planes = PACK // len(bank[i])
-            for n, part in enumerate(bank[i]):
-                nc.scalar.copy(out=res[i][:, n * planes : (n + 1) * planes, :], in_=part[:])
+            for n in range(2):
+                nc.scalar.copy(out=res[i][:, 2 * n : 2 * n + 2, :], in_=res_ps[i][n][:])
             nc.sync.dma_start(out=out_rows[:, :, a:b], in_=res[i][:])
 
-        def hand_on(a, b):
-            nc.vector.quantize_mx(
-                out=res_code[:, a:b].bitcast(FP8X4), scales=res_scale[:, a:b], in_=res_bf[:, PACK * a : PACK * b]
-            )
+        def weave_res(i, engine_copy, c0=0, c1=P):
+            a = PIECES[i][0]
+            weave(engine_copy, res_bf[:, PACK * (a + c0) : PACK * (a + c1)], res[i][:, :, c0:c1])
 
-        def store_codes(a, b):
-            nc.sync.dma_start(out=out_words[:, a:b], in_=res_code[:, a:b].bitcast(I32))
+        def quantise_res(a, b):
+            quantise(res_code[:, a:b], res_scale[:, a:b], res_bf[:, PACK * a : PACK * b])
 
-        leave_psum(0, nc.scalar.copy)
-        leave_psum(1, nc.scalar.copy)
-        leave_psum(2, nc.scalar.copy)
-        deal_w2(0, 64)
-        leave_psum(3, nc.scalar.copy)
-        by_order(vector_gather, 0, 0, 256)
-        by_order(vector_gather, 0, 256, 512)
-        for t in range(1, PACK):
-            if t < PACK - 1:
-                leave_psum(t + 3, nc.scalar.copy)
-            by_order(scalar_gather, t, 0, S)
-        nc.scalar.activation(out=own[:], in_=y_ps[5][:], func=COPY, scale=gain[:, 3:4])
-        deal_w2(64, 104)
-        far_tap(0)
-        deal_w2(104, 128)
-        near_tap(0)
-        far_tap(1)
-        own_tap(0)
-        near_tap(1)
-        far_tap(2)
-        own_tap(1)
-        near_tap(2)
-        far_tap(3)
-        own_tap(2)
-        near_tap(3)
-        nc.vector.quantize_mx(out=w2_code[:].bitcast(FP8X4), scales=w2_scale[:], in_=w2_bf[:])
-        for a, b in HALVES:
-            for t in range(3):
-                by_back(scalar_gather, t, a, b)
-        by_back_with_own(0, 128)
-        by_back_with_own(128, 256)
+        for a, b in Z_PARTS:
+            for t in range(LAST):
+                scalar_gather(z_planes(a, b)[:, t, :], rr[t][:], entries(back_sb, a, b))
+        by_back_last_plane(*PIECES[0])
+        by_back_last_plane(PIECES[1][0], PIECES[2][1])
         weave_z(0, nc.vector.tensor_copy)
-        by_back_with_own(256, 384)
         second_product(0)
         weave_z(1, nc.vector.tensor_copy)
-        by_back_with_own(384, 512)
+        by_back_last_plane(*PIECES[3])
         second_product(1)
         weave_z(2, nc.scalar.copy)
         weave_z(3, nc.vector.tensor_copy)
         second_product(2)
         second_product(3)
-        store_res(0)
-        round_stored(0, nc.vector.tensor_copy)
-        store_res(1)
-        round_stored(1, nc.vector.tensor_copy)
+
+        for i in range(2):
+            store_res(i)
+            weave_res(i, nc.vector.tensor_copy)
         store_res(2)
-        hand_on(0, 256)
-        round_stored(2, nc.vector.tensor_copy, 0, 64)
+        quantise_res(*HALVES[0])
+        weave_res(2, nc.vector.tensor_copy, 0, PIECE_2_ON_VECTOR)
         store_res(3)
-        round_stored(2, nc.scalar.copy, 64, P)
-        round_stored(3, nc.vector.tensor_copy)
-        hand_on(256, 384)
-        hand_on(384, 512)
-        store_codes(0, 512)
+        weave_res(2, nc.scalar.copy, PIECE_2_ON_VECTOR, P)
+        weave_res(3, nc.vector.tensor_copy)
+        quantise_res(*PIECES[2])
+        quantise_res(*PIECES[3])
+        nc.sync.dma_start(out=out_words, in_=res_code[:].bitcast(I32))
         for q in range(4):
             queue = nc.sync if q % 2 else nc.scalar
             queue.dma_start(

@@ -43,8 +43,8 @@ def deal(engine_copy, grouped, raw, m0, m1, base=0):
 
 def weave(engine_copy, woven, planes):
     engine_copy(
-        out=woven.rearrange("p (c i t) -> p c t i", i=4, t=PACK),
-        in_=planes.rearrange("p t (c i) -> p c t i", i=4),
+        out=woven.rearrange("p (c i t) -> p c t i", i=2, t=PACK),
+        in_=planes.rearrange("p t (c i) -> p c t i", i=2),
     )
 
 

@@ -29,8 +29,8 @@ X_CUTS = ((0, 256), (256, 384), (384, 512))
 PIECES = ((0, 128), (128, 256), (256, 384), (384, 512))
 Z_PARTS = ((0, 384), (384, 512))
 W1_ON_VECTOR = (32, 64)
-W2_PARTS = ((0, 64), (64, 96), (96, 128))
-W2_CUT = 112
+W2_PARTS = ((0, 64), (64, 128))
+W2_CUT = 104
 PIECE_2_ON_VECTOR = 64
 
 
@@ -83,7 +83,7 @@ def tile_picked_yserial_none_po_kernel(
         scale_table = tile([P, T], U8, "scale_table", tag="table1")
         word_table = [tile([P, T], U32, "word_table%d" % o, tag="table%d" % o) for o in range(PASSES)]
         w1_raw = [tile([P, PACK, H], F32, "w1_raw%d" % o, tag="raw%d" % o) for o in range(PASSES)]
-        w2_tags = ("raw0", "raw1", "table0")
+        w2_tags = ("raw0", "table0")
         w2_raw = [tile([P, PACK, PACK * (m1 - m0)], F32, "w2_raw%d" % m0, tag=w2_tags[h]) for h, (m0, m1) in enumerate(W2_PARTS)]
         taps_sb = keep.tile([P, PACK, 3], F32, name="taps_sb")
         picked_scale = tile([P, S], U8, "picked_scale")
@@ -206,9 +206,8 @@ def tile_picked_yserial_none_po_kernel(
 
         leave_psum(0)
         leave_psum(1)
+        leave_psum(2)
         deal_w2(0, *W2_PARTS[0])
-        leave_psum(2, nc.vector.tensor_copy)
-        deal_w2(1, *W2_PARTS[1])
         leave_psum(bank_of_plane[1])
         by_order(vector_gather, 0)
         for t in range(1, PACK):
@@ -216,9 +215,9 @@ def tile_picked_yserial_none_po_kernel(
                 leave_psum(bank_of_plane[t + 1])
             by_order(scalar_gather, t)
         nc.scalar.activation(out=own_last[:], in_=y_ps[bank_of_plane[LAST]][:], func=COPY, scale=gain[:, LAST : LAST + 1])
-        deal_w2(2, W2_PARTS[2][0], W2_CUT)
+        deal_w2(1, W2_PARTS[1][0], W2_CUT)
         far_tap(0)
-        deal_w2(2, W2_CUT, P)
+        deal_w2(1, W2_CUT, P)
         near_tap(0)
         for t in range(1, PACK):
             far_tap(t)

@@ -62,7 +62,7 @@ def tile_picked_yserial_none_po_kernel(
         psum = ctx.enter_context(tc.psum_pool(name="psum", bufs=1))
 
         def tile(shape, dtype, name, tag=None):
-            return keep.tile(shape, dtype, name=name, tag=tag or name, align_bytes=64)
+            return keep.tile(shape, dtype, name=name, tag=tag or name, align_bytes=256)
 
         def scalar_cast(out, in_):
             nc.scalar.activation(out=out, in_=in_, func=COPY)

@@ -22,7 +22,7 @@ PASSES = K // (P * PACK)
 LAST = PACK - 1
 PER_COLUMN = 16
 
-Y_WINDOW = (704, 528, 528, 528)
+Y_WINDOW = (512, 528, 528, 512)
 LEAD = 4
 HALVES = ((0, S // 2), (S // 2, S))
 X_CUTS = ((0, 256), (256, 384), (384, 512))
@@ -30,7 +30,6 @@ PIECES = ((0, 128), (128, 256), (256, 384), (384, 512))
 Z_PARTS = ((0, 384), (384, 512))
 W1_ON_VECTOR = (32, 64)
 W2_PARTS = ((0, 64), (64, 128))
-W2_CUT = 104
 PIECE_2_ON_VECTOR = 64
 
 
@@ -59,10 +58,14 @@ def tile_picked_yserial_none_po_kernel(
     with ExitStack() as ctx:
         lists = ctx.enter_context(tc.tile_pool(name="lists", bufs=1))
         keep = ctx.enter_context(tc.tile_pool(name="keep", bufs=1))
+        shared = ctx.enter_context(tc.tile_pool(name="shared", bufs=1))
         psum = ctx.enter_context(tc.psum_pool(name="psum", bufs=1))
 
         def tile(shape, dtype, name, tag=None):
             return keep.tile(shape, dtype, name=name, tag=tag or name, align_bytes=256)
+
+        def tile_at(shape, dtype, name, offset):
+            return shared.tile(shape, dtype, name=name, offset=offset, align_bytes=256)
 
         def scalar_cast(out, in_):
             nc.scalar.activation(out=out, in_=in_, func=COPY)
@@ -81,10 +84,9 @@ def tile_picked_yserial_none_po_kernel(
         back_sb = lists.tile([P, S // PER_COLUMN], U16, name="back_sb")
 
         scale_table = tile([P, T], U8, "scale_table", tag="table1")
-        word_table = [tile([P, T], U32, "word_table%d" % o, tag="table%d" % o) for o in range(PASSES)]
+        word_table = [tile_at([P, T], U32, "word_table0", 0), tile([P, T], U32, "word_table1", tag="table1")]
         w1_raw = [tile([P, PACK, H], F32, "w1_raw%d" % o, tag="raw%d" % o) for o in range(PASSES)]
-        w2_tags = ("raw0", "table0")
-        w2_raw = [tile([P, PACK, PACK * (m1 - m0)], F32, "w2_raw%d" % m0, tag=w2_tags[h]) for h, (m0, m1) in enumerate(W2_PARTS)]
+        w2_raw = [tile([P, PACK, N // 2], F32, "w2_raw0", tag="raw0"), tile_at([P, PACK, N // 2], F32, "w2_raw1", 0)]
         taps_sb = keep.tile([P, PACK, 3], F32, name="taps_sb")
         picked_scale = tile([P, S], U8, "picked_scale")
         x_scale = tile([P, PASSES, S], U8, "x_scale")
@@ -119,19 +121,20 @@ def tile_picked_yserial_none_po_kernel(
             nc.sync.dma_start(out=w2_raw[h][:], in_=w2_rows[:, :, PACK * m0 : PACK * m1])
         nc.sync.dma_start(out=back_sb[:], in_=back)
 
-        y = [tile([P, Y_WINDOW[t]], F32, "y%d" % t) for t in range(PACK)]
+        y = [tile([P, Y_WINDOW[t]], F32, "y%d" % t, tag="y0" if t == LAST else None) for t in range(PACK)]
         gg = [tile([P, LEAD + S], F32, "gg%d" % t) for t in range(PACK)]
         for t in range(PACK):
-            nc.vector.memset(y[t][:, S : Y_WINDOW[t]], 0.0)
+            if 0 < t < LAST:
+                nc.vector.memset(y[t][:, S : Y_WINDOW[t]], 0.0)
             nc.vector.memset(gg[t][:, LEAD - 2 : LEAD], 0.0)
 
         x_code = [tile([P, S], U32, "x_code%d" % o) for o in range(PASSES)]
         w1_code = [tile([P, H], U32, "w1_code%d" % o) for o in range(PASSES)]
         w1_scale = [tile([P, H], U8, "w1_scale%d" % o) for o in range(PASSES)]
         w1_bf = [tile([P, PACK * H], BF16, "w1_bf%d" % o) for o in range(PASSES)]
-        y_banks = [(0, a, b) for a, b in X_CUTS] + [(t, 0, S) for t in range(1, PACK)]
+        y_banks = [(0, a, b) for a, b in X_CUTS] + [(1, a, b) for a, b in HALVES] + [(2, 0, S), (3, 0, S)]
         y_ps = [psum.tile([P, b - a], F32, name="y_ps%d" % n, tag="y_ps%d" % n) for n, (t, a, b) in enumerate(y_banks)]
-        bank_of_plane = {t: n for n, (t, a, b) in enumerate(y_banks) if t > 0}
+        bank_of_plane = {t: n for n, (t, a, b) in enumerate(y_banks) if a == 0}
         w2_bf = tile([P, PACK * N], BF16, "w2_bf")
 
         def first_product(o, n, a, b):
@@ -151,7 +154,7 @@ def tile_picked_yserial_none_po_kernel(
             deal(nc.vector.tensor_copy, w1_bf[o], w1_raw[o], 0, W1_ON_VECTOR[o])
             deal(scalar_cast, w1_bf[o], w1_raw[o], W1_ON_VECTOR[o], P)
             quantise(w1_code[o][:], w1_scale[o][:], w1_bf[o][:])
-        for a, b in HALVES:
+        for a, b in ((0, 128), (128, 256), (256, 512)):
             vector_gather(x_code[0][:, a:b], word_table[0][:], entries(offs_sb, a, b))
             for n, (t, first, end) in enumerate(y_banks):
                 if first < b and end > a:
@@ -162,15 +165,14 @@ def tile_picked_yserial_none_po_kernel(
             for n, (first, end) in enumerate(X_CUTS):
                 if a <= first and end <= b:
                     first_product(1, n, first, end)
-            first_product(1, bank_of_plane[1], a, b)
+            first_product(1, bank_of_plane[1] + a // HALVES[0][1], a, b)
         for t in range(2, PACK):
             first_product(1, bank_of_plane[t], 0, S)
 
         gain = keep.tile([P, PACK], F32, name="gain")
         nc.scalar.activation(out=gain[:], in_=taps_sb[:, :, 0], func=COPY, bias=1.0)
 
-        far_tags = ("far0", "table0", "near0", "near1")
-        far = [tile([P, S], F32, "far%d" % t, tag=far_tags[t]) for t in range(PACK)]
+        far = [tile_at([P, S], F32, "far%d" % t, 4 * S * (t % 2)) for t in range(LAST)] + [tile([P, S], F32, "far3", tag="near1")]
         near = [tile([P, S], F32, "near%d" % t) for t in range(LAST)]
         own_last = tile([P, S], F32, "own_last")
         rr = [tile([P, S], F32, "rr%d" % t) for t in range(PACK)]
@@ -181,8 +183,8 @@ def tile_picked_yserial_none_po_kernel(
             t, a, b = y_banks[n]
             engine_copy(out=y[t][:, a:b], in_=y_ps[n][:])
 
-        def by_order(gather, t):
-            gather(gg[t][:, LEAD : LEAD + S], y[t][:], order_sb[:])
+        def by_order(gather, t, a=0, b=S):
+            gather(gg[t][:, LEAD + a : LEAD + b], y[t][:], entries(order_sb, a, b))
 
         def shifted(t, steps):
             return gg[t][:, LEAD - steps : LEAD - steps + S]
@@ -201,28 +203,41 @@ def tile_picked_yserial_none_po_kernel(
                 out=rr[t][:], in0=shifted(t, 0), scalar=gain[:, t : t + 1], in1=near[t][:], op0=MULT, op1=ADD
             )
 
-        def deal_w2(h, m0, m1):
-            deal(nc.vector.tensor_copy, w2_bf, w2_raw[h], m0, m1, base=W2_PARTS[h][0])
+        for h, (m0, m1) in enumerate(W2_PARTS):
+            nc.gpsimd.tensor_scalar(
+                out=w2_bf[:].rearrange("p (t m j) -> p m t j", t=PACK, j=PACK)[:, m0:m1],
+                in0=w2_raw[h][:].rearrange("p j (m t) -> p m t j", t=PACK),
+                scalar1=1.0,
+                scalar2=0.0,
+                op0=MULT,
+                op1=ADD,
+            )
 
         leave_psum(0)
         leave_psum(1)
+        leave_psum(bank_of_plane[1], nc.vector.tensor_copy)
         leave_psum(2)
-        deal_w2(0, *W2_PARTS[0])
-        leave_psum(bank_of_plane[1])
-        by_order(vector_gather, 0)
-        for t in range(1, PACK):
-            if t < LAST:
-                leave_psum(bank_of_plane[t + 1])
-            by_order(scalar_gather, t)
+        leave_psum(bank_of_plane[1] + 1)
+        by_order(vector_gather, 0, 0, S - P)
+        by_order(scalar_gather, 0, S - P, S)
+        leave_psum(bank_of_plane[2], nc.vector.tensor_copy)
+        by_order(scalar_gather, 1)
+        leave_psum(bank_of_plane[3])
+        by_order(scalar_gather, 2)
+        by_order(scalar_gather, 3, 0, S - P)
+        by_order(scalar_gather, 3, S - P, S)
         nc.scalar.activation(out=own_last[:], in_=y_ps[bank_of_plane[LAST]][:], func=COPY, scale=gain[:, LAST : LAST + 1])
-        deal_w2(1, W2_PARTS[1][0], W2_CUT)
         far_tap(0)
-        deal_w2(1, W2_CUT, P)
+        far_tap(1)
         near_tap(0)
-        for t in range(1, PACK):
-            far_tap(t)
-            own_tap(t - 1)
-            near_tap(t)
+        near_tap(1)
+        own_tap(0)
+        far_tap(2)
+        own_tap(1)
+        near_tap(2)
+        far_tap(3)
+        own_tap(2)
+        near_tap(3)
         quantise(w2_code[:], w2_scale[:], w2_bf[:])
 
         z = [tile([P, PACK, b - a], F32, "z%d" % a, tag="near1" if a else None) for a, b in Z_PARTS]
@@ -235,7 +250,7 @@ def tile_picked_yserial_none_po_kernel(
         res_scale = tile([P, S], U8, "res_scale")
         out_rows = out_0.rearrange("(p t) j -> p t j", t=PACK)
         out_words = out_1[0].rearrange("p c r -> p (c r)").bitcast(I32)
-        res_tags = ["res_ps0", "res_ps1"] + ["y_ps%d" % n for n in range(len(y_banks))]
+        res_tags = ["res_ps0"] + ["y_ps%d" % n for n in range(len(y_banks))]
         res_ps = [
             [psum.tile([P, 2, P], F32, name="res_ps%d_%d" % (i, n), tag=res_tags[2 * i + n]) for n in range(2)]
             for i in range(len(PIECES))

@@ -29,7 +29,7 @@ X_CUTS = ((0, 256), (256, 384), (384, 512))
 PIECES = ((0, 128), (128, 256), (256, 384), (384, 512))
 Z_PARTS = ((0, 384), (384, 512))
 W1_ON_VECTOR = (32, 64)
-W2_PARTS = ((0, 64), (64, 128))
+W2_PARTS = ((0, 56), (56, 104), (104, 128))
 PIECE_2_ON_VECTOR = 64
 
 
@@ -86,7 +86,12 @@ def tile_picked_yserial_none_po_kernel(
         scale_table = tile([P, T], U8, "scale_table", tag="table1")
         word_table = [tile_at([P, T], U32, "word_table0", 0), tile([P, T], U32, "word_table1", tag="table1")]
         w1_raw = [tile([P, PACK, H], F32, "w1_raw%d" % o, tag="raw%d" % o) for o in range(PASSES)]
-        w2_raw = [tile([P, PACK, N // 2], F32, "w2_raw0", tag="raw0"), tile_at([P, PACK, N // 2], F32, "w2_raw1", 0)]
+        w2_shapes = [[P, PACK, PACK * (m1 - m0)] for m0, m1 in W2_PARTS]
+        w2_raw = [
+            tile(w2_shapes[0], F32, "w2_raw0", tag="raw0"),
+            tile_at(w2_shapes[1], F32, "w2_raw1", 1024),
+            tile_at(w2_shapes[2], F32, "w2_raw2", 4096),
+        ]
         taps_sb = keep.tile([P, PACK, 3], F32, name="taps_sb")
         picked_scale = tile([P, S], U8, "picked_scale")
         x_scale = tile([P, PASSES, S], U8, "x_scale")
@@ -203,7 +208,7 @@ def tile_picked_yserial_none_po_kernel(
                 out=rr[t][:], in0=shifted(t, 0), scalar=gain[:, t : t + 1], in1=near[t][:], op0=MULT, op1=ADD
             )
 
-        for h, (m0, m1) in enumerate(W2_PARTS):
+        for h, (m0, m1) in enumerate(W2_PARTS[:2]):
             nc.gpsimd.tensor_scalar(
                 out=w2_bf[:].rearrange("p (t m j) -> p m t j", t=PACK, j=PACK)[:, m0:m1],
                 in0=w2_raw[h][:].rearrange("p j (m t) -> p m t j", t=PACK),
@@ -231,6 +236,7 @@ def tile_picked_yserial_none_po_kernel(
         far_tap(1)
         near_tap(0)
         near_tap(1)
+        deal(nc.vector.tensor_copy, w2_bf, w2_raw[2], *W2_PARTS[2], base=W2_PARTS[2][0])
         own_tap(0)
         far_tap(2)
         own_tap(1)

@@ -22,7 +22,7 @@ PASSES = K // (P * PACK)
 LAST = PACK - 1
 PER_COLUMN = 16
 
-Y_WINDOW = (512, 528, 528, 512)
+Y_WINDOW = (608, 528, 528, 512)
 LEAD = 4
 HALVES = ((0, S // 2), (S // 2, S))
 X_CUTS = ((0, 256), (256, 384), (384, 512))
@@ -129,7 +129,7 @@ def tile_picked_yserial_none_po_kernel(
         y = [tile([P, Y_WINDOW[t]], F32, "y%d" % t, tag="y0" if t == LAST else None) for t in range(PACK)]
         gg = [tile([P, LEAD + S], F32, "gg%d" % t) for t in range(PACK)]
         for t in range(PACK):
-            if 0 < t < LAST:
+            if t < LAST:
                 nc.vector.memset(y[t][:, S : Y_WINDOW[t]], 0.0)
             nc.vector.memset(gg[t][:, LEAD - 2 : LEAD], 0.0)
 
@@ -137,7 +137,7 @@ def tile_picked_yserial_none_po_kernel(
         w1_code = [tile([P, H], U32, "w1_code%d" % o) for o in range(PASSES)]
         w1_scale = [tile([P, H], U8, "w1_scale%d" % o) for o in range(PASSES)]
         w1_bf = [tile([P, PACK * H], BF16, "w1_bf%d" % o) for o in range(PASSES)]
-        y_banks = [(0, a, b) for a, b in X_CUTS] + [(1, a, b) for a, b in HALVES] + [(2, 0, S), (3, 0, S)]
+        y_banks = [(0, a, b) for a, b in X_CUTS] + [(t, a, b) for t in (1, 2) for a, b in HALVES] + [(3, 0, S)]
         y_ps = [psum.tile([P, b - a], F32, name="y_ps%d" % n, tag="y_ps%d" % n) for n, (t, a, b) in enumerate(y_banks)]
         bank_of_plane = {t: n for n, (t, a, b) in enumerate(y_banks) if a == 0}
         w2_bf = tile([P, PACK * N], BF16, "w2_bf")
@@ -170,9 +170,9 @@ def tile_picked_yserial_none_po_kernel(
             for n, (first, end) in enumerate(X_CUTS):
                 if a <= first and end <= b:
                     first_product(1, n, first, end)
-            first_product(1, bank_of_plane[1] + a // HALVES[0][1], a, b)
-        for t in range(2, PACK):
-            first_product(1, bank_of_plane[t], 0, S)
+            for t in (1, 2):
+                first_product(1, bank_of_plane[t] + a // HALVES[0][1], a, b)
+        first_product(1, bank_of_plane[LAST], 0, S)
 
         gain = keep.tile([P, PACK], F32, name="gain")
         nc.scalar.activation(out=gain[:], in_=taps_sb[:, :, 0], func=COPY, bias=1.0)
@@ -221,11 +221,12 @@ def tile_picked_yserial_none_po_kernel(
         leave_psum(0)
         leave_psum(1)
         leave_psum(bank_of_plane[1], nc.vector.tensor_copy)
+        leave_psum(bank_of_plane[2], nc.vector.tensor_copy)
         leave_psum(2)
         leave_psum(bank_of_plane[1] + 1)
-        by_order(vector_gather, 0, 0, S - P)
-        by_order(scalar_gather, 0, S - P, S)
-        leave_psum(bank_of_plane[2], nc.vector.tensor_copy)
+        by_order(vector_gather, 0, 0, 448)
+        by_order(scalar_gather, 0, 448, S)
+        leave_psum(bank_of_plane[2] + 1, nc.vector.tensor_copy)
         by_order(scalar_gather, 1)
         leave_psum(bank_of_plane[3])
         by_order(scalar_gather, 2)
@@ -256,7 +257,7 @@ def tile_picked_yserial_none_po_kernel(
         res_scale = tile([P, S], U8, "res_scale")
         out_rows = out_0.rearrange("(p t) j -> p t j", t=PACK)
         out_words = out_1[0].rearrange("p c r -> p (c r)").bitcast(I32)
-        res_tags = ["res_ps0"] + ["y_ps%d" % n for n in range(len(y_banks))]
+        res_tags = ["y_ps%d" % n for n in range(len(y_banks))]
         res_ps = [
             [psum.tile([P, 2, P], F32, name="res_ps%d_%d" % (i, n), tag=res_tags[2 * i + n]) for n in range(2)]
             for i in range(len(PIECES))

@@ -25,12 +25,17 @@ PER_COLUMN = 16
 Y_WINDOW = (608, 528, 528, 512)
 LEAD = 4
 HALVES = ((0, S // 2), (S // 2, S))
+FIRST_CUTS = ((0, 128), (128, 256), (256, 512))
 X_CUTS = ((0, 256), (256, 384), (384, 512))
 PIECES = ((0, 128), (128, 256), (256, 384), (384, 512))
 Z_PARTS = ((0, 384), (384, 512))
 W1_ON_VECTOR = (32, 64)
 W2_PARTS = ((0, 56), (56, 104), (104, 128))
+ORDER_ON_VECTOR = 448
 PIECE_2_ON_VECTOR = 64
+FAR_BYTES = 4 * S
+W2_SECOND_AT = FAR_BYTES // 2
+W2_THIRD_AT = 2 * FAR_BYTES
 
 
 def deal(engine_copy, grouped, raw, m0, m1, base=0):
@@ -83,16 +88,16 @@ def tile_picked_yserial_none_po_kernel(
         order_sb = lists.tile([P, S // PER_COLUMN], U16, name="order_sb")
         back_sb = lists.tile([P, S // PER_COLUMN], U16, name="back_sb")
 
-        scale_table = tile([P, T], U8, "scale_table", tag="table1")
-        word_table = [tile_at([P, T], U32, "word_table0", 0), tile([P, T], U32, "word_table1", tag="table1")]
+        scale_table = tile_at([P, T], U8, "scale_table", 4 * T)
+        word_table = [tile_at([P, T], U32, "word_table%d" % o, (4 * T + 256) * o) for o in range(PASSES)]
         w1_raw = [tile([P, PACK, H], F32, "w1_raw%d" % o, tag="raw%d" % o) for o in range(PASSES)]
         w2_shapes = [[P, PACK, PACK * (m1 - m0)] for m0, m1 in W2_PARTS]
         w2_raw = [
             tile(w2_shapes[0], F32, "w2_raw0", tag="raw0"),
-            tile_at(w2_shapes[1], F32, "w2_raw1", 1024),
-            tile_at(w2_shapes[2], F32, "w2_raw2", 4096),
+            tile_at(w2_shapes[1], F32, "w2_raw1", W2_SECOND_AT),
+            tile_at(w2_shapes[2], F32, "w2_raw2", W2_THIRD_AT),
         ]
-        taps_sb = keep.tile([P, PACK, 3], F32, name="taps_sb")
+        taps_sb = tile_at([P, PACK, 3], F32, "taps_sb", 4 * T)
         picked_scale = tile([P, S], U8, "picked_scale")
         x_scale = tile([P, PASSES, S], U8, "x_scale")
 
@@ -112,8 +117,6 @@ def tile_picked_yserial_none_po_kernel(
         nc.sync.dma_start(out=offs_sb[:], in_=offs)
         nc.sync.dma_start(out=w1_raw[1][:], in_=w1_rows[1])
         load_words(0)
-        nc.sync.dma_start(out=taps_sb[:], in_=taps.rearrange("(p t) e -> p t e", t=PACK))
-        nc.sync.dma_start(out=order_sb[:], in_=order)
         vector_gather(picked_scale[:], scale_table[:], offs_sb[:])
         for q in range(4):
             nc.sync.dma_start(
@@ -121,6 +124,8 @@ def tile_picked_yserial_none_po_kernel(
                 in_=picked_scale[32 * q : 32 * q + 32 : 4, :].bitcast(I32),
             )
         load_words(1)
+        nc.sync.dma_start(out=order_sb[:], in_=order)
+        nc.sync.dma_start(out=taps_sb[:], in_=taps.rearrange("(p t) e -> p t e", t=PACK))
         w2_rows = w2.rearrange("(p j) c -> p j c", j=PACK)
         for h, (m0, m1) in enumerate(W2_PARTS):
             nc.sync.dma_start(out=w2_raw[h][:], in_=w2_rows[:, :, PACK * m0 : PACK * m1])
@@ -129,7 +134,7 @@ def tile_picked_yserial_none_po_kernel(
         y = [tile([P, Y_WINDOW[t]], F32, "y%d" % t, tag="y0" if t == LAST else None) for t in range(PACK)]
         gg = [tile([P, LEAD + S], F32, "gg%d" % t) for t in range(PACK)]
         for t in range(PACK):
-            if t < LAST:
+            if Y_WINDOW[t] > S:
                 nc.vector.memset(y[t][:, S : Y_WINDOW[t]], 0.0)
             nc.vector.memset(gg[t][:, LEAD - 2 : LEAD], 0.0)
 
@@ -137,7 +142,7 @@ def tile_picked_yserial_none_po_kernel(
         w1_code = [tile([P, H], U32, "w1_code%d" % o) for o in range(PASSES)]
         w1_scale = [tile([P, H], U8, "w1_scale%d" % o) for o in range(PASSES)]
         w1_bf = [tile([P, PACK * H], BF16, "w1_bf%d" % o) for o in range(PASSES)]
-        y_banks = [(0, a, b) for a, b in X_CUTS] + [(t, a, b) for t in (1, 2) for a, b in HALVES] + [(3, 0, S)]
+        y_banks = [(0, a, b) for a, b in X_CUTS] + [(t, a, b) for t in (1, 2) for a, b in HALVES] + [(LAST, 0, S)]
         y_ps = [psum.tile([P, b - a], F32, name="y_ps%d" % n, tag="y_ps%d" % n) for n, (t, a, b) in enumerate(y_banks)]
         bank_of_plane = {t: n for n, (t, a, b) in enumerate(y_banks) if a == 0}
         w2_bf = tile([P, PACK * N], BF16, "w2_bf")
@@ -159,25 +164,26 @@ def tile_picked_yserial_none_po_kernel(
             deal(nc.vector.tensor_copy, w1_bf[o], w1_raw[o], 0, W1_ON_VECTOR[o])
             deal(scalar_cast, w1_bf[o], w1_raw[o], W1_ON_VECTOR[o], P)
             quantise(w1_code[o][:], w1_scale[o][:], w1_bf[o][:])
-        for a, b in ((0, 128), (128, 256), (256, 512)):
+        for a, b in FIRST_CUTS:
             vector_gather(x_code[0][:, a:b], word_table[0][:], entries(offs_sb, a, b))
             for n, (t, first, end) in enumerate(y_banks):
                 if first < b and end > a:
                     first_product(0, n, max(a, first), min(b, end))
         for a, b in X_CUTS:
             vector_gather(x_code[1][:, a:b], word_table[1][:], entries(offs_sb, a, b))
-        for a, b in HALVES:
+        for h, (a, b) in enumerate(HALVES):
             for n, (first, end) in enumerate(X_CUTS):
                 if a <= first and end <= b:
                     first_product(1, n, first, end)
             for t in (1, 2):
-                first_product(1, bank_of_plane[t] + a // HALVES[0][1], a, b)
+                first_product(1, bank_of_plane[t] + h, a, b)
         first_product(1, bank_of_plane[LAST], 0, S)
 
         gain = keep.tile([P, PACK], F32, name="gain")
         nc.scalar.activation(out=gain[:], in_=taps_sb[:, :, 0], func=COPY, bias=1.0)
 
-        far = [tile_at([P, S], F32, "far%d" % t, 4 * S * (t % 2)) for t in range(LAST)] + [tile([P, S], F32, "far3", tag="near1")]
+        far = [tile_at([P, S], F32, "far%d" % t, FAR_BYTES * (t % 2)) for t in range(LAST)]
+        far.append(tile([P, S], F32, "far%d" % LAST, tag="near1"))
         near = [tile([P, S], F32, "near%d" % t) for t in range(LAST)]
         own_last = tile([P, S], F32, "own_last")
         rr = [tile([P, S], F32, "rr%d" % t) for t in range(PACK)]
@@ -218,20 +224,20 @@ def tile_picked_yserial_none_po_kernel(
                 op1=ADD,
             )
 
-        leave_psum(0)
-        leave_psum(1)
+        leave_psum(bank_of_plane[0])
+        leave_psum(bank_of_plane[0] + 1)
         leave_psum(bank_of_plane[1], nc.vector.tensor_copy)
         leave_psum(bank_of_plane[2], nc.vector.tensor_copy)
-        leave_psum(2)
+        leave_psum(bank_of_plane[0] + 2)
         leave_psum(bank_of_plane[1] + 1)
-        by_order(vector_gather, 0, 0, 448)
-        by_order(scalar_gather, 0, 448, S)
+        by_order(vector_gather, 0, 0, ORDER_ON_VECTOR)
+        by_order(scalar_gather, 0, ORDER_ON_VECTOR, S)
         leave_psum(bank_of_plane[2] + 1, nc.vector.tensor_copy)
         by_order(scalar_gather, 1)
-        leave_psum(bank_of_plane[3])
+        leave_psum(bank_of_plane[LAST])
         by_order(scalar_gather, 2)
-        by_order(scalar_gather, 3, 0, S - P)
-        by_order(scalar_gather, 3, S - P, S)
+        by_order(scalar_gather, LAST, 0, S - P)
+        by_order(scalar_gather, LAST, S - P, S)
         nc.scalar.activation(out=own_last[:], in_=y_ps[bank_of_plane[LAST]][:], func=COPY, scale=gain[:, LAST : LAST + 1])
         far_tap(0)
         far_tap(1)
@@ -242,9 +248,9 @@ def tile_picked_yserial_none_po_kernel(
         far_tap(2)
         own_tap(1)
         near_tap(2)
-        far_tap(3)
+        far_tap(LAST)
         own_tap(2)
-        near_tap(3)
+        near_tap(LAST)
         quantise(w2_code[:], w2_scale[:], w2_bf[:])
 
         z = [tile([P, PACK, b - a], F32, "z%d" % a, tag="near1" if a else None) for a, b in Z_PARTS]
@@ -257,9 +263,8 @@ def tile_picked_yserial_none_po_kernel(
         res_scale = tile([P, S], U8, "res_scale")
         out_rows = out_0.rearrange("(p t) j -> p t j", t=PACK)
         out_words = out_1[0].rearrange("p c r -> p (c r)").bitcast(I32)
-        res_tags = ["y_ps%d" % n for n in range(len(y_banks))]
         res_ps = [
-            [psum.tile([P, 2, P], F32, name="res_ps%d_%d" % (i, n), tag=res_tags[2 * i + n]) for n in range(2)]
+            [psum.tile([P, 2, P], F32, name="res_ps%d_%d" % (i, n), tag="y_ps%d" % (2 * i + n)) for n in range(2)]
             for i in range(len(PIECES))
         ]
 

from contextlib import ExitStack

import concourse.mybir as mybir

K, T, S, H, N = 1024, 2048, 512, 512, 512
FLOPS = 2 * K * H * S + 2 * H * N * S

F32 = mybir.dt.float32
BF16 = mybir.dt.bfloat16
I32 = mybir.dt.int32
U32 = mybir.dt.uint32
U16 = mybir.dt.uint16
U8 = mybir.dt.uint8
FP8X4 = mybir.dt.float8_e4m3fn_x4
COPY = mybir.ActivationFunctionType.Copy
MULT = mybir.AluOpType.mult
ADD = mybir.AluOpType.add

P = 128
PACK = 4
PASSES = K // (P * PACK)
LAST = PACK - 1
PER_COLUMN = 16

Y_WINDOW = (608, 528, 528, 512)
LEAD = 4
HALVES = ((0, S // 2), (S // 2, S))
FIRST_CUTS = ((0, 128), (128, 256), (256, 512))
X_CUTS = ((0, 256), (256, 384), (384, 512))
PIECES = ((0, 128), (128, 256), (256, 384), (384, 512))
Z_PARTS = ((0, 384), (384, 512))
W1_ON_VECTOR = (32, 64)
W2_PARTS = ((0, 56), (56, 104), (104, 128))
ORDER_ON_VECTOR = 448
PIECE_2_ON_VECTOR = 64
FAR_BYTES = 4 * S
W2_SECOND_AT = FAR_BYTES // 2
W2_THIRD_AT = 2 * FAR_BYTES


def deal(engine_copy, grouped, raw, m0, m1, base=0):
    engine_copy(
        out=grouped[:].rearrange("p (t m j) -> p m j t", t=PACK, j=PACK)[:, m0:m1],
        in_=raw[:].rearrange("p j (m t) -> p m j t", t=PACK)[:, m0 - base : m1 - base],
    )


def weave(engine_copy, woven, planes):
    engine_copy(
        out=woven.rearrange("p (c i t) -> p c t i", i=2, t=PACK),
        in_=planes.rearrange("p t (c i) -> p c t i", i=2),
    )


def entries(list_tile, a, b):
    return list_tile[:, a // PER_COLUMN : b // PER_COLUMN]


def tile_picked_yserial_none_po_kernel(
    tc, x_words, x_scales, w1, w2, taps, offs, order, back, out_0, out_1, out_2
):
    nc = tc.nc
    with ExitStack() as ctx:
        lists = ctx.enter_context(tc.tile_pool(name="lists", bufs=1))
        keep = ctx.enter_context(tc.tile_pool(name="keep", bufs=1))
        shared = ctx.enter_context(tc.tile_pool(name="shared", bufs=1))
        psum = ctx.enter_context(tc.psum_pool(name="psum", bufs=1))

        def tile(shape, dtype, name, tag=None):
            return keep.tile(shape, dtype, name=name, tag=tag or name, align_bytes=256)

        def tile_at(shape, dtype, name, offset):
            return shared.tile(shape, dtype, name=name, offset=offset, align_bytes=256)

        def scalar_cast(out, in_):
            nc.scalar.activation(out=out, in_=in_, func=COPY)

        def vector_gather(out, window, offsets):
            nc.vector.tensor_copy(out=out, in_=window.indirect(offsets))

        def scalar_gather(out, window, offsets):
            nc.scalar.activation(out=out, in_=window.indirect(offsets), func=COPY)

        def quantise(code, scale, woven):
            nc.vector.quantize_mx(out=code.bitcast(FP8X4), scales=scale, in_=woven)

        offs_sb = lists.tile([P, S // PER_COLUMN], U16, name="offs_sb")
        order_sb = lists.tile([P, S // PER_COLUMN], U16, name="order_sb")
        back_sb = lists.tile([P, S // PER_COLUMN], U16, name="back_sb")

        scale_table = tile_at([P, T], U8, "scale_table", 4 * T)
        word_table = [tile_at([P, T], U32, "word_table%d" % o, (4 * T + 256) * o) for o in range(PASSES)]
        w1_raw = [tile([P, PACK, H], F32, "w1_raw%d" % o, tag="raw%d" % o) for o in range(PASSES)]
        w2_shapes = [[P, PACK, PACK * (m1 - m0)] for m0, m1 in W2_PARTS]
        w2_raw = [
            tile(w2_shapes[0], F32, "w2_raw0", tag="raw0"),
            tile_at(w2_shapes[1], F32, "w2_raw1", W2_SECOND_AT),
            tile_at(w2_shapes[2], F32, "w2_raw2", W2_THIRD_AT),
        ]
        taps_sb = tile_at([P, PACK, 3], F32, "taps_sb", 4 * T)
        picked_scale = tile([P, S], U8, "picked_scale")
        x_scale = tile([P, PASSES, S], U8, "x_scale")

        nc.vector.memset(scale_table[:, 0 : T // 2].bitcast(I32), 0)
        nc.gpsimd.memset(scale_table[:, T // 2 : T].bitcast(I32), 0)
        nc.gpsimd.memset(x_scale[:].bitcast(I32), 0)
        w1_rows = w1.rearrange("(o p j) c -> o p j c", o=PASSES, j=PACK)

        def load_words(o):
            nc.sync.dma_start(
                out=word_table[o][:].bitcast(I32), in_=x_words[o].rearrange("p c r -> p (c r)").bitcast(I32)
            )

        nc.sync.dma_start(out=w1_raw[0][:], in_=w1_rows[0])
        for o in range(PASSES):
            nc.sync.dma_start(out=scale_table[4 * o : P : 8, :].bitcast(I32), in_=x_scales[o].bitcast(I32))
        nc.sync.dma_start(out=offs_sb[:], in_=offs)
        nc.sync.dma_start(out=w1_raw[1][:], in_=w1_rows[1])
        load_words(0)
        vector_gather(picked_scale[:], scale_table[:], offs_sb[:])
        for q in range(4):
            nc.sync.dma_start(
                out=x_scale[32 * q : 32 * q + 4].rearrange("r o c -> r (o c)").bitcast(I32),
                in_=picked_scale[32 * q : 32 * q + 32 : 4, :].bitcast(I32),
            )
        load_words(1)
        nc.sync.dma_start(out=order_sb[:], in_=order)
        nc.sync.dma_start(out=taps_sb[:], in_=taps.rearrange("(p t) e -> p t e", t=PACK))
        w2_rows = w2.rearrange("(p j) c -> p j c", j=PACK)
        for h, (m0, m1) in enumerate(W2_PARTS):
            nc.sync.dma_start(out=w2_raw[h][:], in_=w2_rows[:, :, PACK * m0 : PACK * m1])
        nc.sync.dma_start(out=back_sb[:], in_=back)

        y = [tile([P, Y_WINDOW[t]], F32, "y%d" % t, tag="y0" if t == LAST else None) for t in range(PACK)]
        gg = [tile([P, LEAD + S], F32, "gg%d" % t) for t in range(PACK)]
        for t in range(PACK):
            if Y_WINDOW[t] > S:
                nc.vector.memset(y[t][:, S : Y_WINDOW[t]], 0.0)
            nc.vector.memset(gg[t][:, LEAD - 2 : LEAD], 0.0)

        x_code = [tile([P, S], U32, "x_code%d" % o) for o in range(PASSES)]
        w1_code = [tile([P, H], U32, "w1_code%d" % o) for o in range(PASSES)]
        w1_scale = [tile([P, H], U8, "w1_scale%d" % o) for o in range(PASSES)]
        w1_bf = [tile([P, PACK * H], BF16, "w1_bf%d" % o) for o in range(PASSES)]
        y_banks = [(0, a, b) for a, b in X_CUTS] + [(t, a, b) for t in (1, 2) for a, b in HALVES] + [(LAST, 0, S)]
        y_ps = [psum.tile([P, b - a], F32, name="y_ps%d" % n, tag="y_ps%d" % n) for n, (t, a, b) in enumerate(y_banks)]
        bank_of_plane = {t: n for n, (t, a, b) in enumerate(y_banks) if a == 0}
        w2_bf = tile([P, PACK * N], BF16, "w2_bf")

        def first_product(o, n, a, b):
            t, first, end = y_banks[n]
            cols = slice(t * P, (t + 1) * P)
            nc.tensor.matmul_mx(
                out=y_ps[n][:, a - first : b - first],
                lhsT=w1_code[o][:, cols].bitcast(FP8X4),
                lhsT_scale=w1_scale[o][:, cols],
                rhs=x_code[o][:, a:b].bitcast(FP8X4),
                rhs_scale=x_scale[:, o, a:b],
                start=(o == 0 and a == first),
                stop=(o == PASSES - 1 and b == end),
            )

        for o in range(PASSES):
            deal(nc.vector.tensor_copy, w1_bf[o], w1_raw[o], 0, W1_ON_VECTOR[o])
            deal(scalar_cast, w1_bf[o], w1_raw[o], W1_ON_VECTOR[o], P)
            quantise(w1_code[o][:], w1_scale[o][:], w1_bf[o][:])
        for a, b in FIRST_CUTS:
            vector_gather(x_code[0][:, a:b], word_table[0][:], entries(offs_sb, a, b))
            for n, (t, first, end) in enumerate(y_banks):
                if first < b and end > a:
                    first_product(0, n, max(a, first), min(b, end))
        for a, b in X_CUTS:
            vector_gather(x_code[1][:, a:b], word_table[1][:], entries(offs_sb, a, b))
        for h, (a, b) in enumerate(HALVES):
            for n, (first, end) in enumerate(X_CUTS):
                if a <= first and end <= b:
                    first_product(1, n, first, end)
            for t in (1, 2):
                first_product(1, bank_of_plane[t] + h, a, b)
        first_product(1, bank_of_plane[LAST], 0, S)

        gain = keep.tile([P, PACK], F32, name="gain")
        nc.scalar.activation(out=gain[:], in_=taps_sb[:, :, 0], func=COPY, bias=1.0)

        far = [tile_at([P, S], F32, "far%d" % t, FAR_BYTES * (t % 2)) for t in range(LAST)]
        far.append(tile([P, S], F32, "far%d" % LAST, tag="near1"))
        near = [tile([P, S], F32, "near%d" % t) for t in range(LAST)]
        own_last = tile([P, S], F32, "own_last")
        rr = [tile([P, S], F32, "rr%d" % t) for t in range(PACK)]
        w2_code = tile([P, N], U32, "w2_code", tag="near2")
        w2_scale = tile([P, N], U8, "w2_scale")

        def leave_psum(n, engine_copy=nc.scalar.copy):
            t, a, b = y_banks[n]
            engine_copy(out=y[t][:, a:b], in_=y_ps[n][:])

        def by_order(gather, t, a=0, b=S):
            gather(gg[t][:, LEAD + a : LEAD + b], y[t][:], entries(order_sb, a, b))

        def shifted(t, steps):
            return gg[t][:, LEAD - steps : LEAD - steps + S]

        def far_tap(t):
            nc.vector.tensor_scalar(out=far[t][:], in0=shifted(t, 2), scalar1=taps_sb[:, t, 2:3], scalar2=None, op0=MULT)

        def near_tap(t):
            total = rr[t] if t == LAST else near[t]
            nc.vector.scalar_tensor_tensor(
                out=total[:], in0=shifted(t, 1), scalar=taps_sb[:, t, 1:2], in1=far[t][:], op0=MULT, op1=ADD
            )

        def own_tap(t):
            nc.vector.scalar_tensor_tensor(
                out=rr[t][:], in0=shifted(t, 0), scalar=gain[:, t : t + 1], in1=near[t][:], op0=MULT, op1=ADD
            )

        for h, (m0, m1) in enumerate(W2_PARTS[:2]):
            nc.gpsimd.tensor_scalar(
                out=w2_bf[:].rearrange("p (t m j) -> p m t j", t=PACK, j=PACK)[:, m0:m1],
                in0=w2_raw[h][:].rearrange("p j (m t) -> p m t j", t=PACK),
                scalar1=1.0,
                scalar2=0.0,
                op0=MULT,
                op1=ADD,
            )

        leave_psum(bank_of_plane[0])
        leave_psum(bank_of_plane[0] + 1)
        leave_psum(bank_of_plane[1], nc.vector.tensor_copy)
        leave_psum(bank_of_plane[2], nc.vector.tensor_copy)
        leave_psum(bank_of_plane[0] + 2)
        leave_psum(bank_of_plane[1] + 1)
        by_order(vector_gather, 0, 0, ORDER_ON_VECTOR)
        by_order(scalar_gather, 0, ORDER_ON_VECTOR, S)
        leave_psum(bank_of_plane[2] + 1, nc.vector.tensor_copy)
        by_order(scalar_gather, 1)
        leave_psum(bank_of_plane[LAST])
        by_order(scalar_gather, 2)
        by_order(scalar_gather, LAST, 0, S - P)
        by_order(scalar_gather, LAST, S - P, S)
        nc.scalar.activation(out=own_last[:], in_=y_ps[bank_of_plane[LAST]][:], func=COPY, scale=gain[:, LAST : LAST + 1])
        far_tap(0)
        far_tap(1)
        near_tap(0)
        near_tap(1)
        deal(nc.vector.tensor_copy, w2_bf, w2_raw[2], *W2_PARTS[2], base=W2_PARTS[2][0])
        own_tap(0)
        far_tap(2)
        own_tap(1)
        near_tap(2)
        far_tap(LAST)
        own_tap(2)
        near_tap(LAST)
        quantise(w2_code[:], w2_scale[:], w2_bf[:])

        z = [tile([P, PACK, b - a], F32, "z%d" % a, tag="near1" if a else None) for a, b in Z_PARTS]
        z_bf = tile([P, PACK * S], BF16, "z_bf")
        z_code = [tile([P, b - a], U32, "z_code%d" % a) for a, b in PIECES]
        z_scale = [tile([P, b - a], U8, "z_scale%d" % a) for a, b in PIECES]
        res = [tile([P, PACK, b - a], F32, "res%d" % a) for a, b in PIECES]
        res_bf = tile([P, PACK * S], BF16, "res_bf")
        res_code = tile([P, S], U32, "res_code")
        res_scale = tile([P, S], U8, "res_scale")
        out_rows = out_0.rearrange("(p t) j -> p t j", t=PACK)
        out_words = out_1[0].rearrange("p c r -> p (c r)").bitcast(I32)
        res_ps = [
            [psum.tile([P, 2, P], F32, name="res_ps%d_%d" % (i, n), tag="y_ps%d" % (2 * i + n)) for n in range(2)]
            for i in range(len(PIECES))
        ]

        def z_planes(a, b):
            part = a // Z_PARTS[1][0]
            return z[part][:, :, a - Z_PARTS[part][0] : b - Z_PARTS[part][0]]

        def by_back_last_plane(a, b):
            nc.vector.tensor_tensor(
                out=z_planes(a, b)[:, LAST, :], in0=rr[LAST][:].indirect(entries(back_sb, a, b)), in1=own_last[:, a:b], op=ADD
            )

        def weave_z(i, engine_copy):
            a, b = PIECES[i]
            weave(engine_copy, z_bf[:, PACK * a : PACK * b], z_planes(a, b))

        def second_product(i):
            a, b = PIECES[i]
            quantise(z_code[i][:], z_scale[i][:], z_bf[:, PACK * a : PACK * b])
            for t in range(PACK):
                cols = slice(t * P, (t + 1) * P)
                nc.tensor.matmul_mx(
                    out=res_ps[i][t // 2][:, t % 2, :],
                    lhsT=w2_code[:, cols].bitcast(FP8X4),
                    lhsT_scale=w2_scale[:, cols],
                    rhs=z_code[i][:].bitcast(FP8X4),
                    rhs_scale=z_scale[i][:],
                    start=True,
                    stop=True,
                )

        def store_res(i):
            a, b = PIECES[i]
            for n in range(2):
                nc.scalar.copy(out=res[i][:, 2 * n : 2 * n + 2, :], in_=res_ps[i][n][:])
            nc.sync.dma_start(out=out_rows[:, :, a:b], in_=res[i][:])

        def weave_res(i, engine_copy, c0=0, c1=P):
            a = PIECES[i][0]
            weave(engine_copy, res_bf[:, PACK * (a + c0) : PACK * (a + c1)], res[i][:, :, c0:c1])

        def quantise_res(a, b):
            quantise(res_code[:, a:b], res_scale[:, a:b], res_bf[:, PACK * a : PACK * b])

        for a, b in Z_PARTS:
            for t in range(LAST):
                scalar_gather(z_planes(a, b)[:, t, :], rr[t][:], entries(back_sb, a, b))
        by_back_last_plane(*PIECES[0])
        by_back_last_plane(PIECES[1][0], PIECES[2][1])
        weave_z(0, nc.vector.tensor_copy)
        second_product(0)
        weave_z(1, nc.vector.tensor_copy)
        by_back_last_plane(*PIECES[3])
        second_product(1)
        weave_z(2, nc.scalar.copy)
        weave_z(3, nc.vector.tensor_copy)
        second_product(2)
        second_product(3)

        for i in range(2):
            store_res(i)
            weave_res(i, nc.vector.tensor_copy)
        store_res(2)
        quantise_res(*HALVES[0])
        weave_res(2, nc.vector.tensor_copy, 0, PIECE_2_ON_VECTOR)
        store_res(3)
        weave_res(2, nc.scalar.copy, PIECE_2_ON_VECTOR, P)
        weave_res(3, nc.vector.tensor_copy)
        quantise_res(*PIECES[2])
        quantise_res(*PIECES[3])
        nc.sync.dma_start(out=out_words, in_=res_code[:].bitcast(I32))
        for q in range(4):
            queue = nc.sync if q % 2 else nc.scalar
            queue.dma_start(
                out=out_2[0, 4 * q : 4 * q + 4, :].bitcast(I32), in_=res_scale[32 * q : 32 * q + 4, :].bitcast(I32)
            )
